import numpy as np
import ml_dtypes


def mxq(x, axis, fmt="e4m3"):
    dtype, down = {"e4m3": (ml_dtypes.float8_e4m3fn, 7), "e5m2": (ml_dtypes.float8_e5m2, 14)}[fmt]
    v = np.moveaxis(np.asarray(x, np.float32).astype(ml_dtypes.bfloat16).astype(np.float64), axis, -1)
    blocks = v.reshape(v.shape[:-1] + (-1, 32))
    amax = np.abs(blocks).max(-1, keepdims=True)
    byte = np.maximum(np.where(amax > 0, np.frexp(amax)[1] - 1 + 127, 0) - down, 1)
    scale = np.exp2(byte - 127.0)
    codes = (blocks / scale).astype(np.float32).astype(dtype).astype(np.float64)
    return np.moveaxis((codes * scale).reshape(v.shape), -1, axis)


WIDE = False


def mx_kscale(k):
    if not WIDE:
        return np.ones(k)
    levels = np.array([10, -10, 5, -5, 0])
    if k % 512:
        return np.exp2(np.random.permutation(np.resize(levels, k // 32))).repeat(32)
    a = np.empty((k // 512, 16))
    for p in range(k // 512):
        a[p, :8] = np.random.permutation(np.resize(levels, 8))
        for g in range(8):
            far = levels[np.abs(levels - a[p, g]) >= 10]
            a[p, g + 8] = far[np.random.randint(len(far))]
    return np.exp2(a.ravel()).repeat(32)


BF16 = ml_dtypes.bfloat16


def bf(x):
    return np.asarray(x, np.float32).astype(BF16)


def f64(x):
    return np.asarray(x).astype(np.float64)


E2M1 = np.array([0.0, 0.5, 1.0, 1.5, 2.0, 3.0, 4.0, 6.0, -0.0, -0.5, -1.0, -1.5, -2.0, -3.0, -4.0, -6.0])


def pack_weight(w, fmt):
    k, n = w.shape
    w = f64(bf(w)).reshape(k // 32, 32, n)
    amax = np.abs(w).max(1)
    if fmt == "e4m3":
        byte = np.frexp(amax)[1] - 1 + 127 - 7
    else:
        mant, ex = np.frexp(amax / 6.0)
        byte = np.where(mant > 0.5, ex, ex - 1) + 127
    byte = np.clip(np.where(amax > 0, byte, 1), 1, 254)
    scaled = (w * np.exp2(127.0 - byte)[:, None, :]).reshape(k, n).astype(np.float32)
    by_word = np.ascontiguousarray(scaled.reshape(k // 512, 128, 4, n).transpose(0, 1, 3, 2))
    if fmt == "e4m3":
        words = by_word.astype(ml_dtypes.float8_e4m3fn).view(np.uint8)
    else:
        c = by_word.astype(ml_dtypes.float4_e2m1fn).view(np.uint8) & 0xF
        words = c[..., 0::2] | (c[..., 1::2] << 4)
    return np.ascontiguousarray(words), np.ascontiguousarray(byte.astype(np.uint8).reshape(k // 512, 16, n))


def unpack_weight(words, scales, fmt):
    g, p, n, _ = words.shape
    if fmt == "e4m3":
        vals = np.ascontiguousarray(words).view(ml_dtypes.float8_e4m3fn).astype(np.float64)
    else:
        nib = np.empty((g, p, n, 4), np.uint8)
        nib[..., 0::2] = words & 0xF
        nib[..., 1::2] = words >> 4
        vals = E2M1[nib]
    vals = vals * np.repeat(np.exp2(scales.astype(np.float64) - 127.0), 8, axis=1)[..., None]
    return vals.transpose(0, 1, 3, 2).reshape(g * 512, n)

def planes(Y):
    n, m = Y.shape
    b = f64(bf(Y)).reshape(n // 32, 32, m)
    amax = np.abs(b).max(1)
    byte = np.clip(np.where(amax > 0, np.frexp(amax)[1] - 1 + 127 - 7, 1), 1, 254)
    codes = (b * np.exp2(127.0 - byte)[:, None, :]).reshape(n, m).astype(np.float32).astype(ml_dtypes.float8_e4m3fn).view(np.uint8)
    words = codes.reshape(n // 512, 128, 4, m).transpose(0, 1, 3, 2)
    return np.ascontiguousarray(words), np.ascontiguousarray(byte.astype(np.uint8).reshape(n // 512, 16, m))


B, D, X = 1024, 1024, 512


def _euler(state, z):
    return state + 0.5 * (np.tanh(z) - 0.5 * state)


def setup_inputs():
    s, t = mx_kscale(X), mx_kscale(D)
    h = bf(np.random.standard_normal((B, D)) * 0.5)
    x = bf(np.random.standard_normal((B, X)) * s)
    w = bf(np.random.standard_normal((D, D)) * np.sqrt(2.0 / D))
    win_words, win_scales = pack_weight(np.random.standard_normal((X, D)) / np.sqrt(X) / s[:, None], "e4m3")
    return {"h": h,
            "x": x,
            "w": w,
            "win_words": win_words,
            "win_scales": win_scales,
            "b": bf(np.random.standard_normal(D) * 0.3),
            "p": bf((1.0 + 0.25 * np.random.standard_normal(D)) * t),
            "r": bf((1.0 + 0.25 * np.random.standard_normal(D)) / t)}


def core(h, x, w, win_words, win_scales, b, p, r):
    h, w, b, p, r = f64(h), f64(w), f64(b), f64(p), f64(r)
    a = mxq(r[:, None] * (w - w.T), 0, "e4m3")
    c = (mxq(f64(x), 1, "e4m3") @ unpack_weight(win_words, win_scales, "e4m3")) + b[None, :]
    z1 = (mxq(h * p[None, :], 1, "e4m3") @ a) + c
    u1 = _euler(h, z1)
    z2 = (mxq(u1 * p[None, :], 1, "e4m3") @ a) + c
    return 0.5 * h + 0.5 * _euler(u1, z2)


def reference(h, x, w, win_words, win_scales, b, p, r):
    R_out = core(h, x, w, win_words, win_scales, b, p, r)
    words, scales = planes(R_out.T)
    return R_out, words, scales

@@ -1,0 +1,545 @@
+from contextlib import ExitStack
+
+import concourse.mybir as mybir
+from concourse.masks import make_identity
+
+B, D, X = 1024, 1024, 512
+FLOPS = 2 * B * D * (X + 2 * D)
+
+F32 = mybir.dt.float32
+BF16 = mybir.dt.bfloat16
+I32 = mybir.dt.int32
+U32 = mybir.dt.uint32
+U8 = mybir.dt.uint8
+FP8X4 = mybir.dt.float8_e4m3fn_x4
+ACT = mybir.ActivationFunctionType
+ALU = mybir.AluOpType
+
+P = 128
+PACK = 4
+GROUP = P * PACK
+GROUPS = D // GROUP
+CHUNKS = [(0, 256), (256, 512), (768, 256)]
+HALF = 256
+
+
+def tile_antisymmetricssprk2step_x2_kernel(tc, h, x, w, win_words, win_scales, b, p, r, out_0, out_1, out_2):
+    nc = tc.nc
+    with ExitStack() as ctx:
+        keep = ctx.enter_context(tc.tile_pool(name="keep", bufs=1))
+        work = ctx.enter_context(tc.tile_pool(name="work", bufs=2))
+        psum = ctx.enter_context(tc.psum_pool(name="psum", bufs=8))
+
+        def new_bank():
+            return psum.tile([P, 512], F32, name="bank")
+
+        def quantize(codes, scales, values):
+            nc.vector.quantize_mx(out=codes.bitcast(FP8X4), scales=scales, in_=values)
+
+        ident = keep.tile([P, P], F32, name="ident")
+        make_identity(nc, ident[:])
+        warm = keep.tile([P, 1], F32, name="warm")
+        nc.scalar.activation(out=warm[:], in_=ident[:, 0:1], func=ACT.Tanh)
+
+        w_quad = {}
+        h_rows = {}
+        x_rows = {}
+
+        def load_w(g, gc):
+            w_quad[g, gc] = keep.tile([P, PACK, GROUP], BF16, name="w_%d_%d" % (g, gc))
+            nc.sync.dma_start(
+                out=w_quad[g, gc][:],
+                in_=w[g * GROUP:(g + 1) * GROUP, gc * GROUP:(gc + 1) * GROUP].rearrange("(p j) n -> p j n", j=PACK),
+            )
+
+        def load_h(q):
+            h_rows[q] = keep.tile([P, 2, D], BF16, name="h_%d" % q)
+            nc.sync.dma_start(out=h_rows[q][:], in_=h[q * HALF:(q + 1) * HALF, :].rearrange("(i p) d -> p i d", p=P))
+
+        def load_x(q):
+            x_rows[q] = keep.tile([P, 2, X], BF16, name="x_%d" % q)
+            nc.sync.dma_start(out=x_rows[q][:], in_=x[q * HALF:(q + 1) * HALF, :].rearrange("(i p) k -> p i k", p=P))
+
+        def load_vector(engine, vec, name):
+            t = keep.tile([P, GROUPS, PACK], BF16, name=name)
+            engine.dma_start(out=t[:], in_=vec.rearrange("(g p t) -> p g t", g=GROUPS, t=PACK))
+            return t
+
+        load_w(0, 0)
+        r_bf = load_vector(nc.scalar, r, "r_bf")
+        p_bf = load_vector(nc.scalar, p, "p_bf")
+        b_bf = load_vector(nc.scalar, b, "b_bf")
+        win_raw_scales = keep.tile([P, D], U8, name="win_raw_scales", align_bytes=64)
+        nc.vector.memset(win_raw_scales[:].bitcast(I32), 0)
+        for quad in range(4):
+            nc.gpsimd.dma_start(
+                out=win_raw_scales[32 * quad:32 * quad + 4, :].bitcast(I32),
+                in_=win_scales[0, 4 * quad:4 * quad + 4, :].bitcast(I32),
+            )
+        win_raw = keep.tile([P, D], I32, name="win_raw")
+
+        def load_win():
+            nc.sync.dma_start(out=win_raw[:], in_=win_words[0].rearrange("p n t -> p (n t)").bitcast(I32))
+
+        load_h(0)
+        load_w(1, 0)
+        load_w(0, 1)
+        load_win()
+        load_x(0)
+        load_h(1)
+        load_x(1)
+        load_w(1, 1)
+        load_h(2)
+        load_x(2)
+        load_h(3)
+        load_x(3)
+
+        r_f32 = keep.tile([P, GROUPS, PACK], F32, name="r_f32")
+        nc.vector.tensor_copy(out=r_f32[:], in_=r_bf[:])
+        b_f32 = keep.tile([P, GROUPS, PACK], F32, name="b_f32")
+        nc.vector.tensor_copy(out=b_f32[:], in_=b_bf[:])
+        half_p = keep.tile([P, GROUPS * PACK, 2], F32, name="half_p")
+        nc.vector.tensor_scalar(
+            out=half_p[:],
+            in0=p_bf[:].rearrange("p g t -> p (g t)").unsqueeze(2).to_broadcast([P, GROUPS * PACK, 2]),
+            scalar1=0.5, scalar2=None, op0=ALU.mult,
+        )
+
+        win_codes = keep.tile([P, D], I32, name="win_codes", align_bytes=64)
+        win_plane = keep.tile([P, D], U8, name="win_plane", align_bytes=64)
+
+        def win_move_codes():
+            nc.vector.tensor_copy(
+                out=win_codes[:].rearrange("p (g t m) -> p g t m", g=GROUPS, t=PACK),
+                in_=win_raw[:].rearrange("p (g m t) -> p g t m", g=GROUPS, t=PACK),
+            )
+
+        def win_move_scales():
+            nc.vector.tensor_copy(
+                out=win_plane[:].rearrange("p (g t m) -> p g t m", g=GROUPS, t=PACK),
+                in_=win_raw_scales[:].rearrange("p (g m t) -> p g t m", g=GROUPS, t=PACK),
+            )
+
+        a_codes = keep.tile([P, GROUPS, D], U32, name="a_codes", align_bytes=64)
+        a_plane = keep.tile([P, GROUPS, D], U8, name="a_plane", align_bytes=64)
+        x_codes = keep.tile([P, B], U32, name="x_codes", align_bytes=64)
+        x_plane = keep.tile([P, B], U8, name="x_plane", align_bytes=64)
+        s_codes = {}
+        s_plane = {}
+        for stage in range(2):
+            s_codes[stage] = keep.tile([P, GROUPS, B], U32, name="s_codes_%d" % stage, align_bytes=64)
+            s_plane[stage] = keep.tile([P, GROUPS, B], U8, name="s_plane_%d" % stage, align_bytes=64)
+        out_plane = keep.tile([P, GROUPS, B], U8, name="out_plane", align_bytes=64)
+
+        w_banks = {}
+        rw = {}
+        rwt = {}
+        a_bf = {}
+
+        def a_turn(g, gc):
+            words = w_quad[gc, g][:].bitcast(F32)
+            for u in range(2):
+                w_banks[g, gc, u] = new_bank()
+                for t in range(PACK):
+                    nc.tensor.transpose(w_banks[g, gc, u][:, t * P:(t + 1) * P], words[:, t, u::2], ident[:])
+
+        def a_direct(g, gc, on_vector):
+            rw[g, gc] = work.tile([P, PACK, GROUP], F32, name="rw", tag="wide", bufs=5)
+            for j in range(PACK):
+                dst = rw[g, gc][:, j, :].rearrange("p (t m) -> p t m", t=PACK)
+                src = w_quad[g, gc][:, j, :].rearrange("p (m t) -> p t m", t=PACK)
+                if on_vector:
+                    nc.vector.tensor_scalar(out=dst, in0=src, scalar1=r_f32[:, g, j:j + 1], scalar2=None, op0=ALU.mult)
+                else:
+                    nc.scalar.activation(out=dst, in_=src, func=ACT.Copy, scale=r_f32[:, g, j:j + 1])
+
+        def a_turned(g, gc):
+            rwt[g, gc] = work.tile([P, PACK, GROUP], F32, name="rwt", tag="wide", bufs=5)
+            for j in range(PACK):
+                nc.scalar.activation(
+                    out=rwt[g, gc][:, j, :],
+                    in_=w_banks[g, gc, j // 2][:].bitcast(BF16).rearrange("p (c e) -> p c e", e=2)[:, :, j % 2],
+                    func=ACT.Copy, scale=r_f32[:, g, j:j + 1],
+                )
+
+        def a_subtract(g, gc):
+            a_bf[g, gc] = work.tile([P, GROUP * PACK], BF16, name="a_bf", tag="staged", bufs=6, align_bytes=64)
+            nc.vector.tensor_tensor(
+                out=a_bf[g, gc][:].rearrange("p (c i j) -> p c j i", i=2, j=PACK),
+                in0=rw[g, gc][:].rearrange("p j (c i) -> p c j i", i=2),
+                in1=rwt[g, gc][:].rearrange("p j (c i) -> p c j i", i=2),
+                op=ALU.subtract,
+            )
+
+        def a_quantize(g, gc):
+            cols = slice(gc * GROUP, (gc + 1) * GROUP)
+            quantize(a_codes[:, g, cols], a_plane[:, g, cols], a_bf[g, gc][:])
+
+        def place(q):
+            for c, (first, width) in enumerate(CHUNKS):
+                if first <= q * HALF < first + width:
+                    return c, slice(q * HALF - first, (q + 1) * HALF - first)
+
+        def batch(c):
+            return slice(CHUNKS[c][0], CHUNKS[c][0] + CHUNKS[c][1])
+
+        def staged(name, shape, dtype):
+            return work.tile(shape, dtype, name=name, tag="staged", bufs=6, align_bytes=64)
+
+        h_t = {}
+        hp_bf = {}
+        h_banks = {}
+
+        def h_turn(q, g):
+            words = h_rows[q][:].bitcast(F32)
+            h_banks[q, g] = new_bank()
+            for u in range(2):
+                for i in range(2):
+                    slot = 2 * u + i
+                    nc.tensor.transpose(
+                        h_banks[q, g][:, slot * P:(slot + 1) * P], words[:, i, 256 * g + u:256 * (g + 1):2], ident[:]
+                    )
+
+        def h_gain(q, g):
+            c, rows = place(q)
+            if (c, g) not in hp_bf:
+                hp_bf[c, g] = staged("hp_bf", [P, CHUNKS[c][1], PACK], BF16)
+            nc.vector.tensor_tensor(
+                out=hp_bf[c, g][:, rows, :].rearrange("p b (u e) -> p b u e", e=2),
+                in0=h_banks[q, g][:].bitcast(BF16).rearrange("p (u b e) -> p b u e", u=2, e=2),
+                in1=p_bf[:, g, :].rearrange("p (u e) -> p u e", e=2).unsqueeze(1).to_broadcast([P, HALF, 2, 2]),
+                op=ALU.mult,
+            )
+
+        def h_keep(q, g):
+            c, rows = place(q)
+            if (c, g) not in h_t:
+                h_t[c, g] = keep.tile([P, 2, CHUNKS[c][1]], F32, name="h_t_%d_%d" % (c, g))
+            nc.scalar.copy(out=h_t[c, g][:, :, rows], in_=h_banks[q, g][:].rearrange("p (u b) -> p u b", u=2))
+
+        def h_quantize(c, g):
+            quantize(s_codes[0][:, g, batch(c)], s_plane[0][:, g, batch(c)], hp_bf[c, g][:].rearrange("p b t -> p (b t)"))
+
+        x_banks = {}
+        x_bf = {}
+
+        def x_turn(q):
+            words = x_rows[q][:].bitcast(F32)
+            x_banks[q] = new_bank()
+            for u in range(2):
+                for i in range(2):
+                    slot = 2 * u + i
+                    nc.tensor.transpose(x_banks[q][:, slot * P:(slot + 1) * P], words[:, i, u::2], ident[:])
+
+        def x_keep(q):
+            c, rows = place(q)
+            if c not in x_bf:
+                x_bf[c] = staged("x_bf", [P, CHUNKS[c][1], 2], F32)
+            nc.scalar.copy(out=x_bf[c][:, rows, :], in_=x_banks[q][:].rearrange("p (u b) -> p b u", u=2))
+
+        def x_quantize(c):
+            quantize(x_codes[:, batch(c)], x_plane[:, batch(c)], x_bf[c][:].rearrange("p b u -> p (b u)").bitcast(BF16))
+
+        def h_view(c, g, u):
+            return h_t[c, g][:, u, :].bitcast(BF16).rearrange("p (b e) -> p e b", e=2)
+
+        z_banks = {}
+        state = {}
+
+        def z_matmul(stage, c, g, u):
+            cols = batch(c)
+            for t in (2 * u, 2 * u + 1):
+                ch = slice(g * GROUP + t * P, g * GROUP + (t + 1) * P)
+                bank = new_bank()
+                z = bank[:, :CHUNKS[c][1]]
+                z_banks[stage, c, g, t] = z
+                nc.tensor.matmul_mx(
+                    out=z, lhsT=win_codes[:, ch].bitcast(FP8X4), lhsT_scale=win_plane[:, ch],
+                    rhs=x_codes[:, cols].bitcast(FP8X4), rhs_scale=x_plane[:, cols], start=True, stop=False,
+                )
+                for kg in range(GROUPS):
+                    nc.tensor.matmul_mx(
+                        out=z, lhsT=a_codes[:, kg, ch].bitcast(FP8X4), lhsT_scale=a_plane[:, kg, ch],
+                        rhs=s_codes[stage][:, kg, cols].bitcast(FP8X4), rhs_scale=s_plane[stage][:, kg, cols],
+                        start=False, stop=(kg == GROUPS - 1),
+                    )
+
+        def z_tanh(stage, c, g, u):
+            if (stage, c, g) not in state:
+                shape = [P, PACK, CHUNKS[c][1]]
+                if stage == 0:
+                    state[stage, c, g] = keep.tile(shape, F32, name="mid_%d_%d" % (c, g))
+                else:
+                    state[stage, c, g] = work.tile(shape, F32, name="twice", tag="wide", bufs=5)
+            for t in (2 * u, 2 * u + 1):
+                nc.scalar.activation(
+                    out=state[stage, c, g][:, t, :], in_=z_banks[stage, c, g, t], func=ACT.Tanh, bias=b_f32[:, g, t:t + 1]
+                )
+
+        up_bf = {}
+
+        def mid_update(c, g, u):
+            pair = state[0, c, g][:, 2 * u:2 * u + 2, :]
+            nc.vector.scalar_tensor_tensor(out=pair, in0=h_view(c, g, u), scalar=1.5, in1=pair, op0=ALU.mult, op1=ALU.add)
+
+        def mid_gain(c, g):
+            up_bf[c, g] = staged("up_bf", [P, CHUNKS[c][1] * PACK], BF16)
+            nc.vector.tensor_tensor(
+                out=up_bf[c, g][:].rearrange("p (c i t) -> p c t i", i=2, t=PACK),
+                in0=state[0, c, g][:].rearrange("p t (c i) -> p c t i", i=2),
+                in1=half_p[:, g * PACK:(g + 1) * PACK, :].unsqueeze(1).to_broadcast([P, CHUNKS[c][1] // 2, PACK, 2]),
+                op=ALU.mult,
+            )
+
+        def mid_quantize(c, g):
+            quantize(s_codes[1][:, g, batch(c)], s_plane[1][:, g, batch(c)], up_bf[c, g][:])
+
+        def mid_carry(c, g, u):
+            pair = state[0, c, g][:, 2 * u:2 * u + 2, :]
+            nc.vector.scalar_tensor_tensor(out=pair, in0=pair, scalar=0.375, in1=h_view(c, g, u), op0=ALU.mult, op1=ALU.add)
+
+        out_bf = {}
+        out_banks = {}
+
+        def out_update(c, g, u):
+            pair = state[1, c, g][:, 2 * u:2 * u + 2, :]
+            nc.vector.scalar_tensor_tensor(
+                out=pair, in0=pair, scalar=0.5, in1=state[0, c, g][:, 2 * u:2 * u + 2, :], op0=ALU.mult, op1=ALU.add
+            )
+
+        def out_round(c, g, on_vector):
+            out_bf[c, g] = staged("out_bf", [P, CHUNKS[c][1] * PACK], BF16)
+            dst = out_bf[c, g][:].rearrange("p (c i t) -> p c t i", i=2, t=PACK)
+            src = state[1, c, g][:].rearrange("p t (c i) -> p c t i", i=2)
+            if on_vector:
+                nc.vector.tensor_scalar(out=dst, in0=src, scalar1=0.5, scalar2=None, op0=ALU.mult)
+            else:
+                nc.scalar.activation(out=dst, in_=src, func=ACT.Copy, scale=0.5)
+
+        def out_planes(c, g):
+            codes = work.tile([P, CHUNKS[c][1]], U32, name="out_codes", align_bytes=64)
+            quantize(codes[:], out_plane[:, g, batch(c)], out_bf[c, g][:])
+            nc.sync.dma_start(
+                out=out_1[g].rearrange("p m t -> p (m t)").bitcast(I32)[:, batch(c)], in_=codes[:].bitcast(I32)
+            )
+
+        def out_scales(g):
+            for quad in range(4):
+                nc.sync.dma_start(
+                    out=out_2[g, 4 * quad:4 * quad + 4, :].bitcast(I32),
+                    in_=out_plane[32 * quad:32 * quad + 4, g, :].bitcast(I32),
+                )
+
+        def out_turn(q, g):
+            c, rows = place(q)
+            for i in range(2):
+                out_banks[q, g, i] = new_bank()
+                first = rows.start + i * P
+                for t in range(PACK):
+                    nc.tensor.transpose(
+                        out_banks[q, g, i][:, t * P:(t + 1) * P], state[1, c, g][:, t, first:first + P], ident[:]
+                    )
+
+        def out_store(q, g):
+            rows = work.tile([P, 2, GROUP], F32, name="out_rows", bufs=4)
+            for i in range(2):
+                nc.scalar.activation(
+                    out=rows[:, i, :].rearrange("p (m t) -> p m t", t=PACK),
+                    in_=out_banks[q, g, i][:].rearrange("p (t m) -> p m t", t=PACK),
+                    func=ACT.Copy, scale=0.5,
+                )
+            nc.sync.dma_start(
+                out=out_0[q * HALF:(q + 1) * HALF, g * GROUP:(g + 1) * GROUP].rearrange("(i p) d -> p i d", p=P),
+                in_=rows[:],
+            )
+
+        ctx.enter_context(tc.manual_schedule())
+        a_direct(0, 0, True)
+        a_turn(0, 0)
+        h_turn(0, 0)
+        a_turn(1, 0)
+        a_direct(1, 0, True)
+        a_turned(0, 0)
+        a_direct(0, 1, False)
+        h_turn(0, 1)
+        h_turn(1, 0)
+        a_turned(1, 0)
+        a_turn(0, 1)
+        win_move_scales()
+        a_subtract(0, 0)
+        h_gain(0, 0)
+        a_turned(0, 1)
+        a_quantize(0, 0)
+        h_gain(0, 1)
+        x_turn(0)
+        x_keep(0)
+        h_gain(1, 0)
+        a_subtract(1, 0)
+        h_quantize(0, 1)
+        h_keep(1, 0)
+        a_subtract(0, 1)
+        h_turn(1, 1)
+        x_turn(1)
+        a_turn(1, 1)
+        a_quantize(1, 0)
+        win_move_codes()
+        h_turn(2, 1)
+        h_turn(2, 0)
+        h_gain(1, 1)
+        a_turned(1, 1)
+        x_turn(2)
+        h_gain(2, 0)
+        x_keep(1)
+        a_direct(1, 1, False)
+        h_turn(3, 1)
+        h_quantize(0, 0)
+        h_keep(2, 0)
+        x_keep(2)
+        h_keep(0, 0)
+        x_quantize(0)
+        z_matmul(0, 0, 0, 0)
+        h_gain(2, 1)
+        h_quantize(1, 0)
+        x_turn(3)
+        h_turn(3, 0)
+        x_keep(3)
+        a_subtract(1, 1)
+        a_quantize(0, 1)
+        a_quantize(1, 1)
+        h_keep(1, 1)
+        z_tanh(0, 0, 0, 0)
+        z_matmul(0, 0, 0, 1)
+        z_matmul(0, 0, 1, 0)
+        h_quantize(1, 1)
+        h_gain(3, 0)
+        x_quantize(2)
+        z_tanh(0, 0, 1, 0)
+        z_matmul(0, 0, 1, 1)
+        z_tanh(0, 0, 0, 1)
+        x_quantize(1)
+        h_gain(3, 1)
+        mid_update(0, 0, 0)
+        z_matmul(0, 1, 1, 0)
+        z_tanh(0, 0, 1, 1)
+        z_matmul(0, 1, 0, 0)
+        mid_update(0, 0, 1)
+        h_keep(0, 1)
+        mid_update(0, 1, 1)
+        h_keep(3, 1)
+        mid_update(0, 1, 0)
+        h_quantize(2, 1)
+        z_tanh(0, 1, 1, 0)
+        mid_gain(0, 1)
+        h_keep(2, 1)
+        z_matmul(0, 1, 1, 1)
+        mid_gain(0, 0)
+        h_quantize(2, 0)
+        mid_quantize(0, 1)
+        z_matmul(0, 1, 0, 1)
+        z_tanh(0, 1, 0, 0)
+        h_keep(3, 0)
+        z_matmul(0, 2, 0, 0)
+        mid_update(1, 0, 0)
+        mid_carry(0, 1, 1)
+        z_tanh(0, 1, 1, 1)
+        mid_update(1, 1, 1)
+        mid_update(1, 1, 0)
+        z_tanh(0, 1, 0, 1)
+        mid_quantize(0, 0)
+        z_matmul(1, 0, 0, 0)
+        mid_carry(0, 1, 0)
+        mid_carry(0, 0, 0)
+        z_matmul(1, 0, 1, 1)
+        z_matmul(0, 2, 1, 0)
+        mid_update(1, 0, 1)
+        mid_carry(0, 0, 1)
+        z_tanh(0, 2, 0, 0)
+        mid_gain(1, 1)
+        mid_gain(1, 0)
+        z_matmul(1, 0, 1, 0)
+        mid_quantize(1, 1)
+        z_tanh(1, 0, 0, 0)
+        z_tanh(0, 2, 1, 0)
+        mid_quantize(1, 0)
+        z_matmul(0, 2, 1, 1)
+        z_matmul(0, 2, 0, 1)
+        mid_update(2, 0, 0)
+        z_tanh(1, 0, 1, 0)
+        z_tanh(0, 2, 1, 1)
+        z_tanh(1, 0, 1, 1)
+        z_matmul(1, 0, 0, 1)
+        z_matmul(1, 1, 0, 0)
+        out_update(0, 0, 0)
+        mid_update(2, 1, 1)
+        z_tanh(0, 2, 0, 1)
+        out_update(0, 1, 0)
+        z_tanh(1, 0, 0, 1)
+        z_matmul(1, 1, 1, 0)
+        out_update(0, 1, 1)
+        mid_update(2, 1, 0)
+        z_tanh(1, 1, 0, 0)
+        mid_update(2, 0, 1)
+        z_tanh(1, 1, 1, 0)
+        z_matmul(1, 1, 0, 1)
+        out_round(0, 1, False)
+        mid_carry(1, 1, 0)
+        out_update(0, 0, 1)
+        z_matmul(1, 1, 1, 1)
+        mid_carry(1, 1, 1)
+        mid_gain(2, 0)
+        mid_gain(2, 1)
+        z_tanh(1, 1, 0, 1)
+        mid_quantize(2, 0)
+        z_tanh(1, 1, 1, 1)
+        out_turn(0, 1)
+        mid_quantize(2, 1)
+        out_turn(0, 0)
+        out_update(1, 1, 1)
+        out_round(0, 0, False)
+        out_update(1, 1, 0)
+        z_matmul(1, 2, 1, 0)
+        out_store(0, 1)
+        mid_carry(1, 0, 0)
+        z_matmul(1, 2, 0, 0)
+        z_matmul(1, 2, 1, 1)
+        out_store(0, 0)
+        out_turn(1, 1)
+        z_tanh(1, 2, 1, 0)
+        mid_carry(1, 0, 1)
+        out_planes(0, 1)
+        z_tanh(1, 2, 0, 0)
+        out_update(1, 0, 0)
+        z_tanh(1, 2, 1, 1)
+        out_turn(2, 1)
+        out_planes(0, 0)
+        out_update(1, 0, 1)
+        mid_carry(2, 1, 1)
+        out_round(1, 1, False)
+        out_store(2, 1)
+        mid_carry(2, 1, 0)
+        out_update(2, 1, 1)
+        out_store(1, 1)
+        z_matmul(1, 2, 0, 1)
+        z_tanh(1, 2, 0, 1)
+        out_update(2, 1, 0)
+        out_turn(2, 0)
+        out_turn(1, 0)
+        out_planes(1, 1)
+        out_round(2, 1, True)
+        mid_carry(2, 0, 1)
+        out_turn(3, 1)
+        mid_carry(2, 0, 0)
+        out_store(2, 0)
+        out_planes(2, 1)
+        out_update(2, 0, 0)
+        out_store(1, 0)
+        out_scales(1)
+        out_store(3, 1)
+        out_update(2, 0, 1)
+        out_turn(3, 0)
+        out_round(1, 0, False)
+        out_planes(1, 0)
+        out_store(3, 0)
+        out_round(2, 0, False)
+        out_planes(2, 0)
+        out_scales(0)

@@ -45,12 +45,12 @@ def tile_antisymmetricssprk2step_x2_kernel(tc, h, x, w, win_words, win_scales, b
         h_rows = {}
         x_rows = {}
 
-        def load_w(g, gc):
+        def load_w(g, gc, pieces=1):
             w_quad[g, gc] = keep.tile([P, PACK, GROUP], BF16, name="w_%d_%d" % (g, gc))
-            nc.sync.dma_start(
-                out=w_quad[g, gc][:],
-                in_=w[g * GROUP:(g + 1) * GROUP, gc * GROUP:(gc + 1) * GROUP].rearrange("(p j) n -> p j n", j=PACK),
-            )
+            rows = w[g * GROUP:(g + 1) * GROUP, gc * GROUP:(gc + 1) * GROUP].rearrange("(p j) n -> p j n", j=PACK)
+            step = PACK // pieces
+            for j in range(0, PACK, step):
+                nc.sync.dma_start(out=w_quad[g, gc][:, j:j + step, :], in_=rows[:, j:j + step, :])
 
         def load_h(q):
             h_rows[q] = keep.tile([P, 2, D], BF16, name="h_%d" % q)
@@ -65,44 +65,48 @@ def tile_antisymmetricssprk2step_x2_kernel(tc, h, x, w, win_words, win_scales, b
             engine.dma_start(out=t[:], in_=vec.rearrange("(g p t) -> p g t", g=GROUPS, t=PACK))
             return t
 
-        load_w(0, 0)
+        load_w(0, 0, 2)
         r_bf = load_vector(nc.scalar, r, "r_bf")
         p_bf = load_vector(nc.scalar, p, "p_bf")
-        b_bf = load_vector(nc.scalar, b, "b_bf")
         win_raw_scales = keep.tile([P, D], U8, name="win_raw_scales", align_bytes=64)
         nc.vector.memset(win_raw_scales[:].bitcast(I32), 0)
-        for quad in range(4):
-            nc.gpsimd.dma_start(
-                out=win_raw_scales[32 * quad:32 * quad + 4, :].bitcast(I32),
-                in_=win_scales[0, 4 * quad:4 * quad + 4, :].bitcast(I32),
-            )
+
+        def load_win_scales():
+            for quad in range(4):
+                nc.sync.dma_start(
+                    out=win_raw_scales[32 * quad:32 * quad + 4, :].bitcast(I32),
+                    in_=win_scales[0, 4 * quad:4 * quad + 4, :].bitcast(I32),
+                )
+
         win_raw = keep.tile([P, D], I32, name="win_raw")
 
         def load_win():
             nc.sync.dma_start(out=win_raw[:], in_=win_words[0].rearrange("p n t -> p (n t)").bitcast(I32))
 
-        load_h(0)
         load_w(1, 0)
         load_w(0, 1)
-        load_win()
+        load_h(0)
         load_x(0)
+        load_win()
+        load_win_scales()
         load_h(1)
         load_x(1)
-        load_w(1, 1)
+        b_bf = load_vector(nc.sync, b, "b_bf")
         load_h(2)
         load_x(2)
+        load_w(1, 1)
         load_h(3)
         load_x(3)
 
         r_f32 = keep.tile([P, GROUPS, PACK], F32, name="r_f32")
         nc.vector.tensor_copy(out=r_f32[:], in_=r_bf[:])
-        b_f32 = keep.tile([P, GROUPS, PACK], F32, name="b_f32")
-        nc.vector.tensor_copy(out=b_f32[:], in_=b_bf[:])
-        half_p = keep.tile([P, GROUPS * PACK, 2], F32, name="half_p")
+        minus_r = keep.tile([P, PACK], F32, name="minus_r")
+        nc.vector.tensor_scalar(out=minus_r[:], in0=r_bf[:, 0, :], scalar1=-1.0, scalar2=None, op0=ALU.mult)
+        gain_p = keep.tile([P, GROUPS * PACK, 2], F32, name="gain_p")
         nc.vector.tensor_scalar(
-            out=half_p[:],
+            out=gain_p[:],
             in0=p_bf[:].rearrange("p g t -> p (g t)").unsqueeze(2).to_broadcast([P, GROUPS * PACK, 2]),
-            scalar1=0.5, scalar2=None, op0=ALU.mult,
+            scalar1=2.0 / 3.0, scalar2=None, op0=ALU.mult,
         )
 
         win_codes = keep.tile([P, D], I32, name="win_codes", align_bytes=64)
@@ -136,16 +140,16 @@ def tile_antisymmetricssprk2step_x2_kernel(tc, h, x, w, win_words, win_scales, b
         rwt = {}
         a_bf = {}
 
-        def a_turn(g, gc):
+        def a_turn(g, gc, u):
             words = w_quad[gc, g][:].bitcast(F32)
-            for u in range(2):
-                w_banks[g, gc, u] = new_bank()
-                for t in range(PACK):
-                    nc.tensor.transpose(w_banks[g, gc, u][:, t * P:(t + 1) * P], words[:, t, u::2], ident[:])
+            w_banks[g, gc, u] = new_bank()
+            for t in range(PACK):
+                nc.tensor.transpose(w_banks[g, gc, u][:, t * P:(t + 1) * P], words[:, t, u::2], ident[:])
 
-        def a_direct(g, gc, on_vector):
-            rw[g, gc] = work.tile([P, PACK, GROUP], F32, name="rw", tag="wide", bufs=5)
-            for j in range(PACK):
+        def a_direct(g, gc, u, on_vector):
+            if (g, gc) not in rw:
+                rw[g, gc] = work.tile([P, PACK, GROUP], F32, name="rw", tag="wide", bufs=5)
+            for j in (2 * u, 2 * u + 1):
                 dst = rw[g, gc][:, j, :].rearrange("p (t m) -> p t m", t=PACK)
                 src = w_quad[g, gc][:, j, :].rearrange("p (m t) -> p t m", t=PACK)
                 if on_vector:
@@ -153,13 +157,14 @@ def tile_antisymmetricssprk2step_x2_kernel(tc, h, x, w, win_words, win_scales, b
                 else:
                     nc.scalar.activation(out=dst, in_=src, func=ACT.Copy, scale=r_f32[:, g, j:j + 1])
 
-        def a_turned(g, gc):
-            rwt[g, gc] = work.tile([P, PACK, GROUP], F32, name="rwt", tag="wide", bufs=5)
-            for j in range(PACK):
+        def a_turned(g, gc, u):
+            if (g, gc) not in rwt:
+                rwt[g, gc] = work.tile([P, PACK, GROUP], F32, name="rwt", tag="wide", bufs=5)
+            for e in range(2):
                 nc.scalar.activation(
-                    out=rwt[g, gc][:, j, :],
-                    in_=w_banks[g, gc, j // 2][:].bitcast(BF16).rearrange("p (c e) -> p c e", e=2)[:, :, j % 2],
-                    func=ACT.Copy, scale=r_f32[:, g, j:j + 1],
+                    out=rwt[g, gc][:, 2 * u + e, :],
+                    in_=w_banks[g, gc, u][:].bitcast(BF16).rearrange("p (c e) -> p c e", e=2)[:, :, e],
+                    func=ACT.Copy, scale=r_f32[:, g, 2 * u + e:2 * u + e + 1],
                 )
 
         def a_subtract(g, gc):
@@ -169,6 +174,45 @@ def tile_antisymmetricssprk2step_x2_kernel(tc, h, x, w, win_words, win_scales, b
                 in0=rw[g, gc][:].rearrange("p j (c i) -> p c j i", i=2),
                 in1=rwt[g, gc][:].rearrange("p j (c i) -> p c j i", i=2),
                 op=ALU.subtract,
+            )
+
+        diff = work.tile([P, PACK, GROUP], F32, name="diff", tag="wide", bufs=5)
+        scaled = {}
+        diff_banks = {}
+
+        def diff_subtract(u):
+            nc.vector.tensor_tensor(
+                out=diff[:, 2 * u:2 * u + 2, :].rearrange("p e (t m) -> p e t m", t=PACK),
+                in0=w_quad[1, 0][:, 2 * u:2 * u + 2, :].rearrange("p e (m t) -> p e t m", t=PACK),
+                in1=w_banks[1, 0, u][:].bitcast(BF16).rearrange("p (t m e) -> p e t m", t=PACK, e=2),
+                op=ALU.subtract,
+            )
+
+        def diff_scale(u):
+            if (1, 0) not in scaled:
+                scaled[1, 0] = staged("scaled", [P, PACK, GROUP], BF16)
+            for j in (2 * u, 2 * u + 1):
+                nc.scalar.activation(
+                    out=scaled[1, 0][:, j, :], in_=diff[:, j, :], func=ACT.Copy, scale=r_f32[:, 1, j:j + 1]
+                )
+
+        def diff_turn(j):
+            diff_banks[j] = new_bank()
+            for t in range(PACK):
+                nc.tensor.transpose(diff_banks[j][:, t * P:(t + 1) * P], diff[:, t, j * P:(j + 1) * P], ident[:])
+
+        def diff_turned(j):
+            if (0, 1) not in scaled:
+                scaled[0, 1] = staged("scaled", [P, PACK, GROUP], BF16)
+            nc.scalar.activation(
+                out=scaled[0, 1][:, j, :], in_=diff_banks[j][:], func=ACT.Copy, scale=minus_r[:, j:j + 1]
+            )
+
+        def a_interleave(g, gc):
+            a_bf[g, gc] = staged("a_bf", [P, GROUP * PACK], BF16)
+            nc.vector.tensor_copy(
+                out=a_bf[g, gc][:].rearrange("p (c i j) -> p c j i", i=4, j=PACK),
+                in_=scaled[g, gc][:].rearrange("p j (c i) -> p c j i", i=4),
             )
 
         def a_quantize(g, gc):
@@ -186,7 +230,7 @@ def tile_antisymmetricssprk2step_x2_kernel(tc, h, x, w, win_words, win_scales, b
         def staged(name, shape, dtype):
             return work.tile(shape, dtype, name=name, tag="staged", bufs=6, align_bytes=64)
 
-        h_t = {}
+        mid = {}
         hp_bf = {}
         h_banks = {}
 
@@ -213,9 +257,16 @@ def tile_antisymmetricssprk2step_x2_kernel(tc, h, x, w, win_words, win_scales, b
 
         def h_keep(q, g):
             c, rows = place(q)
-            if (c, g) not in h_t:
-                h_t[c, g] = keep.tile([P, 2, CHUNKS[c][1]], F32, name="h_t_%d_%d" % (c, g))
-            nc.scalar.copy(out=h_t[c, g][:, :, rows], in_=h_banks[q, g][:].rearrange("p (u b) -> p u b", u=2))
+            if (c, g) not in mid:
+                mid[c, g] = keep.tile([P, PACK, CHUNKS[c][1]], F32, name="mid_%d_%d" % (c, g))
+            nc.scalar.activation(
+                out=mid[c, g][:, :, rows].rearrange("p (u e) b -> p u e b", e=2),
+                in_=h_banks[q, g][:].bitcast(BF16).rearrange("p (u b e) -> p u e b", u=2, e=2),
+                func=ACT.Copy, scale=1.125,
+            )
+
+        def h_halve(q):
+            nc.vector.tensor_scalar(out=h_rows[q][:], in0=h_rows[q][:], scalar1=0.5, scalar2=None, op0=ALU.mult)
 
         def h_quantize(c, g):
             quantize(s_codes[0][:, g, batch(c)], s_plane[0][:, g, batch(c)], hp_bf[c, g][:].rearrange("p b t -> p (b t)"))
@@ -240,9 +291,6 @@ def tile_antisymmetricssprk2step_x2_kernel(tc, h, x, w, win_words, win_scales, b
         def x_quantize(c):
             quantize(x_codes[:, batch(c)], x_plane[:, batch(c)], x_bf[c][:].rearrange("p b u -> p (b u)").bitcast(BF16))
 
-        def h_view(c, g, u):
-            return h_t[c, g][:, u, :].bitcast(BF16).rearrange("p (b e) -> p e b", e=2)
-
         z_banks = {}
         state = {}
 
@@ -266,59 +314,92 @@ def tile_antisymmetricssprk2step_x2_kernel(tc, h, x, w, win_words, win_scales, b
 
         def z_tanh(stage, c, g, u):
             if (stage, c, g) not in state:
-                shape = [P, PACK, CHUNKS[c][1]]
-                if stage == 0:
-                    state[stage, c, g] = keep.tile(shape, F32, name="mid_%d_%d" % (c, g))
-                else:
-                    state[stage, c, g] = work.tile(shape, F32, name="twice", tag="wide", bufs=5)
+                state[stage, c, g] = work.tile([P, PACK, CHUNKS[c][1]], F32, name="tanh_z", tag="wide", bufs=5)
             for t in (2 * u, 2 * u + 1):
                 nc.scalar.activation(
-                    out=state[stage, c, g][:, t, :], in_=z_banks[stage, c, g, t], func=ACT.Tanh, bias=b_f32[:, g, t:t + 1]
+                    out=state[stage, c, g][:, t, :], in_=z_banks[stage, c, g, t], func=ACT.Tanh, bias=b_bf[:, g, t:t + 1]
                 )
 
         up_bf = {}
 
         def mid_update(c, g, u):
-            pair = state[0, c, g][:, 2 * u:2 * u + 2, :]
-            nc.vector.scalar_tensor_tensor(out=pair, in0=h_view(c, g, u), scalar=1.5, in1=pair, op0=ALU.mult, op1=ALU.add)
+            pair = mid[c, g][:, 2 * u:2 * u + 2, :]
+            nc.vector.scalar_tensor_tensor(
+                out=pair, in0=state[0, c, g][:, 2 * u:2 * u + 2, :], scalar=0.75, in1=pair, op0=ALU.mult, op1=ALU.add
+            )
 
         def mid_gain(c, g):
             up_bf[c, g] = staged("up_bf", [P, CHUNKS[c][1] * PACK], BF16)
             nc.vector.tensor_tensor(
                 out=up_bf[c, g][:].rearrange("p (c i t) -> p c t i", i=2, t=PACK),
-                in0=state[0, c, g][:].rearrange("p t (c i) -> p c t i", i=2),
-                in1=half_p[:, g * PACK:(g + 1) * PACK, :].unsqueeze(1).to_broadcast([P, CHUNKS[c][1] // 2, PACK, 2]),
+                in0=mid[c, g][:].rearrange("p t (c i) -> p c t i", i=2),
+                in1=gain_p[:, g * PACK:(g + 1) * PACK, :].unsqueeze(1).to_broadcast([P, CHUNKS[c][1] // 2, PACK, 2]),
                 op=ALU.mult,
             )
 
         def mid_quantize(c, g):
             quantize(s_codes[1][:, g, batch(c)], s_plane[1][:, g, batch(c)], up_bf[c, g][:])
 
-        def mid_carry(c, g, u):
-            pair = state[0, c, g][:, 2 * u:2 * u + 2, :]
-            nc.vector.scalar_tensor_tensor(out=pair, in0=pair, scalar=0.375, in1=h_view(c, g, u), op0=ALU.mult, op1=ALU.add)
-
         out_bf = {}
         out_banks = {}
+        out_rows = {}
+        out_words = {}
+        plane_banks = {}
 
-        def out_update(c, g, u):
-            pair = state[1, c, g][:, 2 * u:2 * u + 2, :]
+        def out_turn(q, g, i):
+            c, rows = place(q)
+            out_banks[q, g, i] = new_bank()
+            first = rows.start + i * P
+            for t in range(PACK):
+                slot = out_banks[q, g, i][:, t * P:(t + 1) * P]
+                nc.tensor.matmul(
+                    out=slot, lhsT=mid[c, g][:, t, first:first + P], rhs=ident[:], is_transpose=True, start=True, stop=False
+                )
+                nc.tensor.matmul(
+                    out=slot, lhsT=state[1, c, g][:, t, first:first + P], rhs=ident[:], is_transpose=True, start=False, stop=True
+                )
+
+        def out_update(q, g, i):
+            if (q, g) not in out_rows:
+                out_rows[q, g] = work.tile([P, 2, GROUP], F32, name="out_rows", bufs=4)
             nc.vector.scalar_tensor_tensor(
-                out=pair, in0=pair, scalar=0.5, in1=state[0, c, g][:, 2 * u:2 * u + 2, :], op0=ALU.mult, op1=ALU.add
+                out=out_rows[q, g][:, i, :].rearrange("p (m t) -> p m t", t=PACK),
+                in0=out_banks[q, g, i][:].rearrange("p (t m) -> p m t", t=PACK),
+                scalar=0.25,
+                in1=h_rows[q][:, i, g * GROUP:(g + 1) * GROUP].rearrange("p (m t) -> p m t", t=PACK),
+                op0=ALU.mult, op1=ALU.add,
             )
 
-        def out_round(c, g, on_vector):
-            out_bf[c, g] = staged("out_bf", [P, CHUNKS[c][1] * PACK], BF16)
-            dst = out_bf[c, g][:].rearrange("p (c i t) -> p c t i", i=2, t=PACK)
-            src = state[1, c, g][:].rearrange("p t (c i) -> p c t i", i=2)
+        def out_store(q, g):
+            nc.sync.dma_start(
+                out=out_0[q * HALF:(q + 1) * HALF, g * GROUP:(g + 1) * GROUP].rearrange("(i p) d -> p i d", p=P),
+                in_=out_rows[q, g][:],
+            )
+
+        def out_round(q, g, on_vector):
+            out_words[q, g] = work.tile([P, 2, HALF, 2], BF16, name="out_words", bufs=3)
+            src = out_rows[q, g][:].rearrange("p i (m u e) -> p u (i m) e", u=2, e=2)
             if on_vector:
-                nc.vector.tensor_scalar(out=dst, in0=src, scalar1=0.5, scalar2=None, op0=ALU.mult)
+                nc.vector.tensor_copy(out=out_words[q, g][:], in_=src)
             else:
-                nc.scalar.activation(out=dst, in_=src, func=ACT.Copy, scale=0.5)
+                nc.scalar.copy(out=out_words[q, g][:], in_=src)
+
+        def plane_turn(q, g):
+            words = out_words[q, g][:].rearrange("p u m e -> p (u m e)").bitcast(F32)
+            plane_banks[q, g] = new_bank()
+            for slot in range(4):
+                cols = slice(slot * P, (slot + 1) * P)
+                nc.tensor.transpose(plane_banks[q, g][:, cols], words[:, cols], ident[:])
+
+        def plane_keep(q, g):
+            c, rows = place(q)
+            if (c, g) not in out_bf:
+                out_bf[c, g] = staged("out_bf", [P, CHUNKS[c][1], 2], F32)
+            nc.scalar.copy(out=out_bf[c, g][:, rows, :], in_=plane_banks[q, g][:].rearrange("p (u b) -> p b u", u=2))
 
         def out_planes(c, g):
             codes = work.tile([P, CHUNKS[c][1]], U32, name="out_codes", align_bytes=64)
-            quantize(codes[:], out_plane[:, g, batch(c)], out_bf[c, g][:])
+            quantize(codes[:], out_plane[:, g, batch(c)], out_bf[c, g][:].rearrange("p b u -> p (b u)").bitcast(BF16))
             nc.sync.dma_start(
                 out=out_1[g].rearrange("p m t -> p (m t)").bitcast(I32)[:, batch(c)], in_=codes[:].bitcast(I32)
             )
@@ -330,216 +411,229 @@ def tile_antisymmetricssprk2step_x2_kernel(tc, h, x, w, win_words, win_scales, b
                     in_=out_plane[32 * quad:32 * quad + 4, g, :].bitcast(I32),
                 )
 
-        def out_turn(q, g):
-            c, rows = place(q)
-            for i in range(2):
-                out_banks[q, g, i] = new_bank()
-                first = rows.start + i * P
-                for t in range(PACK):
-                    nc.tensor.transpose(
-                        out_banks[q, g, i][:, t * P:(t + 1) * P], state[1, c, g][:, t, first:first + P], ident[:]
-                    )
-
-        def out_store(q, g):
-            rows = work.tile([P, 2, GROUP], F32, name="out_rows", bufs=4)
-            for i in range(2):
-                nc.scalar.activation(
-                    out=rows[:, i, :].rearrange("p (m t) -> p m t", t=PACK),
-                    in_=out_banks[q, g, i][:].rearrange("p (t m) -> p m t", t=PACK),
-                    func=ACT.Copy, scale=0.5,
-                )
-            nc.sync.dma_start(
-                out=out_0[q * HALF:(q + 1) * HALF, g * GROUP:(g + 1) * GROUP].rearrange("(i p) d -> p i d", p=P),
-                in_=rows[:],
-            )
-
         ctx.enter_context(tc.manual_schedule())
-        a_direct(0, 0, True)
-        a_turn(0, 0)
-        h_turn(0, 0)
-        a_turn(1, 0)
-        a_direct(1, 0, True)
-        a_turned(0, 0)
-        a_direct(0, 1, False)
+        a_direct(0, 0, 0, False)
+        a_turn(0, 0, 0)
+        a_turn(0, 0, 1)
+        a_turned(0, 0, 0)
+        a_turn(1, 0, 0)
+        a_turned(0, 0, 1)
+        a_direct(0, 0, 1, True)
+        diff_subtract(0)
+        a_turn(1, 0, 1)
+        diff_subtract(1)
         h_turn(0, 1)
-        h_turn(1, 0)
-        a_turned(1, 0)
-        a_turn(0, 1)
-        win_move_scales()
-        a_subtract(0, 0)
-        h_gain(0, 0)
-        a_turned(0, 1)
-        a_quantize(0, 0)
-        h_gain(0, 1)
+        diff_scale(0)
+        diff_scale(1)
         x_turn(0)
+        win_move_scales()
+        diff_turn(3)
+        diff_turn(0)
         x_keep(0)
-        h_gain(1, 0)
-        a_subtract(1, 0)
-        h_quantize(0, 1)
-        h_keep(1, 0)
-        a_subtract(0, 1)
-        h_turn(1, 1)
-        x_turn(1)
-        a_turn(1, 1)
-        a_quantize(1, 0)
+        h_gain(0, 1)
+        diff_turn(2)
+        diff_turn(1)
         win_move_codes()
-        h_turn(2, 1)
-        h_turn(2, 0)
+        a_subtract(0, 0)
+        diff_turned(0)
+        diff_turned(2)
+        a_interleave(1, 0)
+        h_keep(0, 1)
+        diff_turned(1)
+        h_turn(1, 1)
+        h_quantize(0, 1)
         h_gain(1, 1)
-        a_turned(1, 1)
-        x_turn(2)
-        h_gain(2, 0)
-        x_keep(1)
-        a_direct(1, 1, False)
-        h_turn(3, 1)
+        h_turn(0, 0)
+        h_gain(0, 0)
+        diff_turned(3)
+        a_quantize(0, 0)
+        h_turn(2, 0)
         h_quantize(0, 0)
-        h_keep(2, 0)
-        x_keep(2)
-        h_keep(0, 0)
+        h_turn(1, 0)
         x_quantize(0)
-        z_matmul(0, 0, 0, 0)
-        h_gain(2, 1)
-        h_quantize(1, 0)
-        x_turn(3)
-        h_turn(3, 0)
-        x_keep(3)
-        a_subtract(1, 1)
+        a_interleave(0, 1)
+        a_quantize(1, 0)
+        h_gain(1, 0)
+        a_turn(1, 1, 0)
+        a_direct(1, 1, 0, False)
+        a_direct(1, 1, 1, False)
+        a_turn(1, 1, 1)
         a_quantize(0, 1)
-        a_quantize(1, 1)
-        h_keep(1, 1)
+        a_turned(1, 1, 0)
+        a_turned(1, 1, 1)
+        h_keep(0, 0)
+        a_subtract(1, 1)
+        h_gain(2, 0)
+        z_matmul(0, 0, 0, 0)
         z_tanh(0, 0, 0, 0)
+        mid_update(0, 0, 0)
+        h_keep(1, 0)
+        x_turn(1)
+        h_turn(2, 1)
+        h_turn(3, 0)
+        x_turn(2)
+        x_keep(1)
+        x_keep(2)
+        x_turn(3)
+        h_turn(3, 1)
+        x_keep(3)
         z_matmul(0, 0, 0, 1)
-        z_matmul(0, 0, 1, 0)
-        h_quantize(1, 1)
-        h_gain(3, 0)
-        x_quantize(2)
-        z_tanh(0, 0, 1, 0)
-        z_matmul(0, 0, 1, 1)
+        h_gain(2, 1)
+        a_quantize(1, 1)
         z_tanh(0, 0, 0, 1)
         x_quantize(1)
-        h_gain(3, 1)
-        mid_update(0, 0, 0)
-        z_matmul(0, 1, 1, 0)
+        z_matmul(0, 0, 1, 0)
+        z_tanh(0, 0, 1, 0)
+        z_matmul(0, 0, 1, 1)
         z_tanh(0, 0, 1, 1)
-        z_matmul(0, 1, 0, 0)
+        h_quantize(1, 0)
+        h_quantize(1, 1)
+        z_matmul(0, 1, 1, 0)
+        h_gain(3, 0)
         mid_update(0, 0, 1)
-        h_keep(0, 1)
-        mid_update(0, 1, 1)
-        h_keep(3, 1)
-        mid_update(0, 1, 0)
-        h_quantize(2, 1)
+        h_keep(2, 0)
         z_tanh(0, 1, 1, 0)
-        mid_gain(0, 1)
-        h_keep(2, 1)
-        z_matmul(0, 1, 1, 1)
+        h_gain(3, 1)
         mid_gain(0, 0)
-        h_quantize(2, 0)
-        mid_quantize(0, 1)
+        mid_update(0, 1, 1)
+        z_matmul(0, 1, 0, 0)
         z_matmul(0, 1, 0, 1)
         z_tanh(0, 1, 0, 0)
-        h_keep(3, 0)
-        z_matmul(0, 2, 0, 0)
-        mid_update(1, 0, 0)
-        mid_carry(0, 1, 1)
-        z_tanh(0, 1, 1, 1)
-        mid_update(1, 1, 1)
-        mid_update(1, 1, 0)
-        z_tanh(0, 1, 0, 1)
+        x_quantize(2)
+        mid_update(0, 1, 0)
+        h_quantize(2, 0)
+        mid_gain(0, 1)
         mid_quantize(0, 0)
-        z_matmul(1, 0, 0, 0)
-        mid_carry(0, 1, 0)
-        mid_carry(0, 0, 0)
-        z_matmul(1, 0, 1, 1)
-        z_matmul(0, 2, 1, 0)
-        mid_update(1, 0, 1)
-        mid_carry(0, 0, 1)
-        z_tanh(0, 2, 0, 0)
-        mid_gain(1, 1)
-        mid_gain(1, 0)
+        z_matmul(0, 1, 1, 1)
+        mid_quantize(0, 1)
+        h_keep(1, 1)
+        h_keep(2, 1)
+        h_quantize(2, 1)
+        z_tanh(0, 1, 0, 1)
+        mid_update(1, 0, 0)
         z_matmul(1, 0, 1, 0)
-        mid_quantize(1, 1)
-        z_tanh(1, 0, 0, 0)
-        z_tanh(0, 2, 1, 0)
-        mid_quantize(1, 0)
-        z_matmul(0, 2, 1, 1)
-        z_matmul(0, 2, 0, 1)
-        mid_update(2, 0, 0)
         z_tanh(1, 0, 1, 0)
-        z_tanh(0, 2, 1, 1)
-        z_tanh(1, 0, 1, 1)
-        z_matmul(1, 0, 0, 1)
-        z_matmul(1, 1, 0, 0)
-        out_update(0, 0, 0)
-        mid_update(2, 1, 1)
+        mid_update(1, 1, 0)
+        z_matmul(0, 2, 0, 0)
+        z_tanh(0, 1, 1, 1)
+        z_tanh(0, 2, 0, 0)
+        z_matmul(0, 2, 0, 1)
         z_tanh(0, 2, 0, 1)
-        out_update(0, 1, 0)
+        z_matmul(1, 0, 1, 1)
+        z_tanh(1, 0, 1, 1)
+        z_matmul(0, 2, 1, 1)
+        mid_update(1, 0, 1)
+        z_matmul(1, 0, 0, 0)
+        mid_update(1, 1, 1)
+        mid_gain(1, 0)
+        z_tanh(1, 0, 0, 0)
+        mid_gain(1, 1)
+        z_matmul(1, 0, 0, 1)
+        mid_quantize(1, 0)
         z_tanh(1, 0, 0, 1)
-        z_matmul(1, 1, 1, 0)
-        out_update(0, 1, 1)
-        mid_update(2, 1, 0)
-        z_tanh(1, 1, 0, 0)
-        mid_update(2, 0, 1)
-        z_tanh(1, 1, 1, 0)
-        z_matmul(1, 1, 0, 1)
-        out_round(0, 1, False)
-        mid_carry(1, 1, 0)
+        mid_quantize(1, 1)
+        h_halve(0)
+        z_matmul(0, 2, 1, 0)
+        out_turn(0, 0, 0)
+        out_update(0, 0, 0)
+        out_turn(0, 0, 1)
         out_update(0, 0, 1)
+        z_tanh(0, 2, 1, 0)
+        z_tanh(0, 2, 1, 1)
+        out_turn(0, 1, 0)
+        out_update(0, 1, 0)
+        out_turn(0, 1, 1)
+        h_keep(3, 0)
+        mid_update(2, 0, 0)
+        h_keep(3, 1)
+        mid_update(2, 0, 1)
         z_matmul(1, 1, 1, 1)
-        mid_carry(1, 1, 1)
-        mid_gain(2, 0)
-        mid_gain(2, 1)
-        z_tanh(1, 1, 0, 1)
-        mid_quantize(2, 0)
-        z_tanh(1, 1, 1, 1)
-        out_turn(0, 1)
-        mid_quantize(2, 1)
-        out_turn(0, 0)
-        out_update(1, 1, 1)
-        out_round(0, 0, False)
-        out_update(1, 1, 0)
-        z_matmul(1, 2, 1, 0)
+        out_update(0, 1, 1)
         out_store(0, 1)
-        mid_carry(1, 0, 0)
-        z_matmul(1, 2, 0, 0)
-        z_matmul(1, 2, 1, 1)
+        mid_gain(2, 0)
+        mid_quantize(2, 0)
+        z_matmul(1, 1, 1, 0)
+        mid_update(2, 1, 1)
+        mid_update(2, 1, 0)
+        mid_gain(2, 1)
+        z_tanh(1, 1, 1, 0)
+        z_tanh(1, 1, 1, 1)
+        out_round(0, 1, False)
+        z_matmul(1, 1, 0, 1)
+        out_round(0, 0, False)
+        z_matmul(1, 1, 0, 0)
+        z_tanh(1, 1, 0, 0)
+        out_turn(1, 1, 1)
+        plane_turn(0, 1)
+        plane_keep(0, 1)
+        mid_quantize(2, 1)
+        z_tanh(1, 1, 0, 1)
+        h_halve(1)
+        out_turn(1, 1, 0)
+        out_update(1, 1, 0)
+        h_halve(2)
+        out_update(1, 1, 1)
         out_store(0, 0)
-        out_turn(1, 1)
+        out_turn(2, 1, 1)
+        z_matmul(1, 2, 1, 0)
         z_tanh(1, 2, 1, 0)
-        mid_carry(1, 0, 1)
+        z_matmul(1, 2, 1, 1)
         out_planes(0, 1)
-        z_tanh(1, 2, 0, 0)
-        out_update(1, 0, 0)
+        plane_turn(0, 0)
         z_tanh(1, 2, 1, 1)
-        out_turn(2, 1)
-        out_planes(0, 0)
-        out_update(1, 0, 1)
-        mid_carry(2, 1, 1)
         out_round(1, 1, False)
-        out_store(2, 1)
-        mid_carry(2, 1, 0)
-        out_update(2, 1, 1)
-        out_store(1, 1)
-        z_matmul(1, 2, 0, 1)
-        z_tanh(1, 2, 0, 1)
+        out_turn(2, 1, 0)
         out_update(2, 1, 0)
-        out_turn(2, 0)
-        out_turn(1, 0)
-        out_planes(1, 1)
-        out_round(2, 1, True)
-        mid_carry(2, 0, 1)
-        out_turn(3, 1)
-        mid_carry(2, 0, 0)
-        out_store(2, 0)
-        out_planes(2, 1)
-        out_update(2, 0, 0)
-        out_store(1, 0)
-        out_scales(1)
-        out_store(3, 1)
-        out_update(2, 0, 1)
-        out_turn(3, 0)
+        out_store(1, 1)
+        out_update(2, 1, 1)
+        out_store(2, 1)
+        out_turn(1, 0, 0)
+        plane_keep(0, 0)
+        out_planes(0, 0)
+        out_turn(1, 0, 1)
+        out_round(2, 1, False)
+        out_update(1, 0, 0)
+        out_turn(2, 0, 0)
+        out_update(1, 0, 1)
         out_round(1, 0, False)
-        out_planes(1, 0)
-        out_store(3, 0)
+        out_turn(3, 1, 1)
+        h_halve(3)
+        plane_turn(1, 1)
+        out_turn(3, 1, 0)
+        out_update(3, 1, 0)
+        out_update(3, 1, 1)
+        plane_keep(1, 1)
+        plane_turn(2, 1)
+        plane_keep(2, 1)
+        z_matmul(1, 2, 0, 1)
+        out_store(1, 0)
+        out_store(3, 1)
+        z_matmul(1, 2, 0, 0)
+        z_tanh(1, 2, 0, 0)
+        z_tanh(1, 2, 0, 1)
+        out_update(2, 0, 0)
+        out_turn(2, 0, 1)
+        out_round(3, 1, True)
+        plane_turn(3, 1)
+        out_turn(3, 0, 0)
+        out_planes(1, 1)
+        plane_keep(3, 1)
+        out_update(2, 0, 1)
         out_round(2, 0, False)
+        out_update(3, 0, 0)
+        out_planes(2, 1)
+        out_turn(3, 0, 1)
+        out_scales(1)
+        plane_turn(1, 0)
+        plane_keep(1, 0)
+        out_update(3, 0, 1)
+        out_round(3, 0, False)
+        out_store(2, 0)
+        plane_turn(2, 0)
+        plane_keep(2, 0)
+        out_store(3, 0)
+        out_planes(1, 0)
+        plane_turn(3, 0)
+        plane_keep(3, 0)
         out_planes(2, 0)
         out_scales(0)

@@ -19,8 +19,8 @@ P = 128
 PACK = 4
 GROUP = P * PACK
 GROUPS = D // GROUP
+QUARTER = 256
 CHUNKS = [(0, 256), (256, 512), (768, 256)]
-HALF = 256
 
 
 def tile_antisymmetricssprk2step_x2_kernel(tc, h, x, w, win_words, win_scales, b, p, r, out_0, out_1, out_2):
@@ -33,8 +33,28 @@ def tile_antisymmetricssprk2step_x2_kernel(tc, h, x, w, win_words, win_scales, b
         def new_bank():
             return psum.tile([P, 512], F32, name="bank")
 
+        def staged(name, shape, dtype):
+            return work.tile(shape, dtype, name=name, tag="staged", bufs=5, align_bytes=64)
+
+        def staged_pair(name, shape):
+            return work.tile(shape, BF16, name=name, tag="staged_pair", bufs=2, align_bytes=64)
+
+        def wide(name, width):
+            return work.tile([P, PACK, width], F32, name=name, tag="wide", bufs=5)
+
         def quantize(codes, scales, values):
             nc.vector.quantize_mx(out=codes.bitcast(FP8X4), scales=scales, in_=values)
+
+        def place(q):
+            for c, (first, width) in enumerate(CHUNKS):
+                if first <= q * QUARTER < first + width:
+                    return c, (q * QUARTER - first) // QUARTER
+
+        def batch(c):
+            return slice(CHUNKS[c][0], CHUNKS[c][0] + CHUNKS[c][1])
+
+        def rows_of(part):
+            return slice(part * QUARTER, (part + 1) * QUARTER)
 
         ident = keep.tile([P, P], F32, name="ident")
         make_identity(nc, ident[:])
@@ -45,7 +65,7 @@ def tile_antisymmetricssprk2step_x2_kernel(tc, h, x, w, win_words, win_scales, b
         h_rows = {}
         x_rows = {}
 
-        def load_w(g, gc, pieces=1):
+        def load_w(g, gc, pieces):
             w_quad[g, gc] = keep.tile([P, PACK, GROUP], BF16, name="w_%d_%d" % (g, gc))
             rows = w[g * GROUP:(g + 1) * GROUP, gc * GROUP:(gc + 1) * GROUP].rearrange("(p j) n -> p j n", j=PACK)
             step = PACK // pieces
@@ -53,23 +73,28 @@ def tile_antisymmetricssprk2step_x2_kernel(tc, h, x, w, win_words, win_scales, b
                 nc.sync.dma_start(out=w_quad[g, gc][:, j:j + step, :], in_=rows[:, j:j + step, :])
 
         def load_h(q):
-            h_rows[q] = keep.tile([P, 2, D], BF16, name="h_%d" % q)
-            nc.sync.dma_start(out=h_rows[q][:], in_=h[q * HALF:(q + 1) * HALF, :].rearrange("(i p) d -> p i d", p=P))
+            c, part = place(q)
+            if c not in h_rows:
+                h_rows[c] = keep.tile([P, CHUNKS[c][1] // P, D], BF16, name="h_%d" % c)
+            nc.sync.dma_start(
+                out=h_rows[c][:, 2 * part:2 * part + 2, :], in_=h[rows_of(q), :].rearrange("(i p) d -> p i d", p=P)
+            )
 
         def load_x(q):
             x_rows[q] = keep.tile([P, 2, X], BF16, name="x_%d" % q)
-            nc.sync.dma_start(out=x_rows[q][:], in_=x[q * HALF:(q + 1) * HALF, :].rearrange("(i p) k -> p i k", p=P))
+            nc.sync.dma_start(out=x_rows[q][:], in_=x[rows_of(q), :].rearrange("(i p) k -> p i k", p=P))
 
         def load_vector(engine, vec, name):
-            t = keep.tile([P, GROUPS, PACK], BF16, name=name)
-            engine.dma_start(out=t[:], in_=vec.rearrange("(g p t) -> p g t", g=GROUPS, t=PACK))
-            return t
+            loaded = keep.tile([P, GROUPS, PACK], BF16, name=name)
+            engine.dma_start(out=loaded[:], in_=vec.rearrange("(g p t) -> p g t", g=GROUPS, t=PACK))
+            return loaded
 
-        load_w(0, 0, 2)
-        r_bf = load_vector(nc.scalar, r, "r_bf")
-        p_bf = load_vector(nc.scalar, p, "p_bf")
-        win_raw_scales = keep.tile([P, D], U8, name="win_raw_scales", align_bytes=64)
+        win_raw = keep.tile([P, D], I32, name="win_raw")
+        win_raw_scales = keep.tile([P, D], U8, name="win_raw_scales")
         nc.vector.memset(win_raw_scales[:].bitcast(I32), 0)
+
+        def load_win():
+            nc.sync.dma_start(out=win_raw[:], in_=win_words[0].rearrange("p n t -> p (n t)").bitcast(I32))
 
         def load_win_scales():
             for quad in range(4):
@@ -78,36 +103,46 @@ def tile_antisymmetricssprk2step_x2_kernel(tc, h, x, w, win_words, win_scales, b
                     in_=win_scales[0, 4 * quad:4 * quad + 4, :].bitcast(I32),
                 )
 
-        win_raw = keep.tile([P, D], I32, name="win_raw")
-
-        def load_win():
-            nc.sync.dma_start(out=win_raw[:], in_=win_words[0].rearrange("p n t -> p (n t)").bitcast(I32))
-
-        load_w(1, 0)
-        load_w(0, 1)
+        r_bf = load_vector(nc.scalar, r, "r_bf")
+        p_bf = load_vector(nc.scalar, p, "p_bf")
+        load_w(0, 0, 2)
         load_h(0)
+        load_w(1, 0, 1)
+        load_w(0, 1, 1)
         load_x(0)
         load_win()
         load_win_scales()
         load_h(1)
+        load_w(1, 1, 1)
         load_x(1)
         b_bf = load_vector(nc.sync, b, "b_bf")
         load_h(2)
         load_x(2)
-        load_w(1, 1)
         load_h(3)
         load_x(3)
 
-        r_f32 = keep.tile([P, GROUPS, PACK], F32, name="r_f32")
-        nc.vector.tensor_copy(out=r_f32[:], in_=r_bf[:])
+        def doubled(vec_bf, factor, name):
+            pairs = keep.tile([P, GROUPS * PACK, 2], F32, name=name)
+            nc.vector.tensor_scalar(
+                out=pairs[:],
+                in0=vec_bf[:].rearrange("p g t -> p (g t)").unsqueeze(2).to_broadcast([P, GROUPS * PACK, 2]),
+                scalar1=factor, scalar2=None, op0=ALU.mult,
+            )
+            return pairs
+
+        r_pairs = doubled(r_bf, 1.0, "r_pairs")
         minus_r = keep.tile([P, PACK], F32, name="minus_r")
         nc.vector.tensor_scalar(out=minus_r[:], in0=r_bf[:, 0, :], scalar1=-1.0, scalar2=None, op0=ALU.mult)
-        gain_p = keep.tile([P, GROUPS * PACK, 2], F32, name="gain_p")
-        nc.vector.tensor_scalar(
-            out=gain_p[:],
-            in0=p_bf[:].rearrange("p g t -> p (g t)").unsqueeze(2).to_broadcast([P, GROUPS * PACK, 2]),
-            scalar1=2.0 / 3.0, scalar2=None, op0=ALU.mult,
-        )
+        gain_pairs = doubled(p_bf, 2.0 / 3.0, "gain_pairs")
+
+        def interleaved(tile_ap, run):
+            return tile_ap.rearrange("p (c i t) -> p c t i", i=run, t=PACK)
+
+        def by_slot(tile_ap, run):
+            return tile_ap.rearrange("p t (c i) -> p c t i", i=run)
+
+        def along(pairs, g, width):
+            return pairs[:, g * PACK:(g + 1) * PACK, :].unsqueeze(1).to_broadcast([P, width // 2, PACK, 2])
 
         win_codes = keep.tile([P, D], I32, name="win_codes", align_bytes=64)
         win_plane = keep.tile([P, D], U8, name="win_plane", align_bytes=64)
@@ -128,17 +163,31 @@ def tile_antisymmetricssprk2step_x2_kernel(tc, h, x, w, win_words, win_scales, b
         a_plane = keep.tile([P, GROUPS, D], U8, name="a_plane", align_bytes=64)
         x_codes = keep.tile([P, B], U32, name="x_codes", align_bytes=64)
         x_plane = keep.tile([P, B], U8, name="x_plane", align_bytes=64)
+        out_plane = keep.tile([P, GROUPS, B], U8, name="out_plane", align_bytes=64)
         s_codes = {}
         s_plane = {}
         for stage in range(2):
-            s_codes[stage] = keep.tile([P, GROUPS, B], U32, name="s_codes_%d" % stage, align_bytes=64)
-            s_plane[stage] = keep.tile([P, GROUPS, B], U8, name="s_plane_%d" % stage, align_bytes=64)
-        out_plane = keep.tile([P, GROUPS, B], U8, name="out_plane", align_bytes=64)
+            for c, (first, width) in enumerate(CHUNKS):
+                s_codes[stage, c] = keep.tile([P, GROUPS, width], U32, name="s_codes_%d_%d" % (stage, c), align_bytes=64)
+                s_plane[stage, c] = keep.tile([P, GROUPS, width], U8, name="s_plane_%d_%d" % (stage, c), align_bytes=64)
+
+        def quantize_state(stage, c, values):
+            quantize(
+                s_codes[stage, c][:].rearrange("p g b -> p (g b)"),
+                s_plane[stage, c][:].rearrange("p g b -> p (g b)"),
+                values[:].rearrange("p g n -> p (g n)"),
+            )
 
         w_banks = {}
         rw = {}
         rwt = {}
+        diff = {}
+        scaled = {}
+        diff_banks = {}
         a_bf = {}
+
+        def r_of(g, j):
+            return r_pairs[:, g * PACK + j, 0:1]
 
         def a_turn(g, gc, u):
             words = w_quad[gc, g][:].bitcast(F32)
@@ -146,60 +195,62 @@ def tile_antisymmetricssprk2step_x2_kernel(tc, h, x, w, win_words, win_scales, b
             for t in range(PACK):
                 nc.tensor.transpose(w_banks[g, gc, u][:, t * P:(t + 1) * P], words[:, t, u::2], ident[:])
 
-        def a_direct(g, gc, u, on_vector):
+        def a_direct(g, gc, u):
             if (g, gc) not in rw:
-                rw[g, gc] = work.tile([P, PACK, GROUP], F32, name="rw", tag="wide", bufs=5)
+                rw[g, gc] = wide("rw", GROUP)
             for j in (2 * u, 2 * u + 1):
-                dst = rw[g, gc][:, j, :].rearrange("p (t m) -> p t m", t=PACK)
-                src = w_quad[g, gc][:, j, :].rearrange("p (m t) -> p t m", t=PACK)
-                if on_vector:
-                    nc.vector.tensor_scalar(out=dst, in0=src, scalar1=r_f32[:, g, j:j + 1], scalar2=None, op0=ALU.mult)
-                else:
-                    nc.scalar.activation(out=dst, in_=src, func=ACT.Copy, scale=r_f32[:, g, j:j + 1])
+                nc.scalar.activation(
+                    out=rw[g, gc][:, j, :].rearrange("p (t m) -> p t m", t=PACK),
+                    in_=w_quad[g, gc][:, j, :].rearrange("p (m t) -> p t m", t=PACK),
+                    func=ACT.Copy, scale=r_of(g, j),
+                )
 
         def a_turned(g, gc, u):
             if (g, gc) not in rwt:
-                rwt[g, gc] = work.tile([P, PACK, GROUP], F32, name="rwt", tag="wide", bufs=5)
+                rwt[g, gc] = wide("rwt", GROUP)
             for e in range(2):
                 nc.scalar.activation(
                     out=rwt[g, gc][:, 2 * u + e, :],
                     in_=w_banks[g, gc, u][:].bitcast(BF16).rearrange("p (c e) -> p c e", e=2)[:, :, e],
-                    func=ACT.Copy, scale=r_f32[:, g, 2 * u + e:2 * u + e + 1],
+                    func=ACT.Copy, scale=r_of(g, 2 * u + e),
                 )
 
         def a_subtract(g, gc):
-            a_bf[g, gc] = work.tile([P, GROUP * PACK], BF16, name="a_bf", tag="staged", bufs=6, align_bytes=64)
+            a_bf[g, gc] = staged("a_bf", [P, GROUP * PACK], BF16)
             nc.vector.tensor_tensor(
-                out=a_bf[g, gc][:].rearrange("p (c i j) -> p c j i", i=2, j=PACK),
-                in0=rw[g, gc][:].rearrange("p j (c i) -> p c j i", i=2),
-                in1=rwt[g, gc][:].rearrange("p j (c i) -> p c j i", i=2),
+                out=interleaved(a_bf[g, gc][:], 2), in0=by_slot(rw[g, gc][:], 2), in1=by_slot(rwt[g, gc][:], 2),
                 op=ALU.subtract,
             )
 
-        diff = work.tile([P, PACK, GROUP], F32, name="diff", tag="wide", bufs=5)
-        scaled = {}
-        diff_banks = {}
-
-        def diff_subtract(u):
+        def diff_subtract(g, gc, u):
+            if (g, gc) not in diff:
+                diff[g, gc] = wide("diff", GROUP)
             nc.vector.tensor_tensor(
-                out=diff[:, 2 * u:2 * u + 2, :].rearrange("p e (t m) -> p e t m", t=PACK),
-                in0=w_quad[1, 0][:, 2 * u:2 * u + 2, :].rearrange("p e (m t) -> p e t m", t=PACK),
-                in1=w_banks[1, 0, u][:].bitcast(BF16).rearrange("p (t m e) -> p e t m", t=PACK, e=2),
+                out=diff[g, gc][:, 2 * u:2 * u + 2, :].rearrange("p e (t m) -> p e t m", t=PACK),
+                in0=w_quad[g, gc][:, 2 * u:2 * u + 2, :].rearrange("p e (m t) -> p e t m", t=PACK),
+                in1=w_banks[g, gc, u][:].bitcast(BF16).rearrange("p (t m e) -> p e t m", t=PACK, e=2),
                 op=ALU.subtract,
             )
 
-        def diff_scale(u):
-            if (1, 0) not in scaled:
-                scaled[1, 0] = staged("scaled", [P, PACK, GROUP], BF16)
+        def diff_gain(g, gc):
+            a_bf[g, gc] = staged("a_bf", [P, GROUP * PACK], BF16)
+            nc.vector.tensor_tensor(
+                out=interleaved(a_bf[g, gc][:], 2), in0=by_slot(diff[g, gc][:], 2), in1=along(r_pairs, g, GROUP),
+                op=ALU.mult,
+            )
+
+        def diff_scale(g, gc, u):
+            if (g, gc) not in scaled:
+                scaled[g, gc] = staged("scaled", [P, PACK, GROUP], BF16)
             for j in (2 * u, 2 * u + 1):
                 nc.scalar.activation(
-                    out=scaled[1, 0][:, j, :], in_=diff[:, j, :], func=ACT.Copy, scale=r_f32[:, 1, j:j + 1]
+                    out=scaled[g, gc][:, j, :], in_=diff[g, gc][:, j, :], func=ACT.Copy, scale=r_of(g, j)
                 )
 
         def diff_turn(j):
             diff_banks[j] = new_bank()
             for t in range(PACK):
-                nc.tensor.transpose(diff_banks[j][:, t * P:(t + 1) * P], diff[:, t, j * P:(j + 1) * P], ident[:])
+                nc.tensor.transpose(diff_banks[j][:, t * P:(t + 1) * P], diff[1, 0][:, t, j * P:(j + 1) * P], ident[:])
 
         def diff_turned(j):
             if (0, 1) not in scaled:
@@ -210,92 +261,82 @@ def tile_antisymmetricssprk2step_x2_kernel(tc, h, x, w, win_words, win_scales, b
 
         def a_interleave(g, gc):
             a_bf[g, gc] = staged("a_bf", [P, GROUP * PACK], BF16)
-            nc.vector.tensor_copy(
-                out=a_bf[g, gc][:].rearrange("p (c i j) -> p c j i", i=4, j=PACK),
-                in_=scaled[g, gc][:].rearrange("p j (c i) -> p c j i", i=4),
-            )
+            nc.vector.tensor_copy(out=interleaved(a_bf[g, gc][:], 4), in_=by_slot(scaled[g, gc][:], 4))
 
         def a_quantize(g, gc):
             cols = slice(gc * GROUP, (gc + 1) * GROUP)
             quantize(a_codes[:, g, cols], a_plane[:, g, cols], a_bf[g, gc][:])
 
-        def place(q):
-            for c, (first, width) in enumerate(CHUNKS):
-                if first <= q * HALF < first + width:
-                    return c, slice(q * HALF - first, (q + 1) * HALF - first)
-
-        def batch(c):
-            return slice(CHUNKS[c][0], CHUNKS[c][0] + CHUNKS[c][1])
-
-        def staged(name, shape, dtype):
-            return work.tile(shape, dtype, name=name, tag="staged", bufs=6, align_bytes=64)
-
         mid = {}
         hp_bf = {}
         h_banks = {}
 
-        def h_turn(q, g):
-            words = h_rows[q][:].bitcast(F32)
-            h_banks[q, g] = new_bank()
+        def turn_words(words_of):
+            bank = new_bank()
             for u in range(2):
                 for i in range(2):
                     slot = 2 * u + i
-                    nc.tensor.transpose(
-                        h_banks[q, g][:, slot * P:(slot + 1) * P], words[:, i, 256 * g + u:256 * (g + 1):2], ident[:]
-                    )
+                    nc.tensor.transpose(bank[:, slot * P:(slot + 1) * P], words_of(i, u), ident[:])
+            return bank
+
+        def h_turn(q, g):
+            c, part = place(q)
+            words = h_rows[c][:].bitcast(F32)
+            h_banks[q, g] = turn_words(lambda i, u: words[:, 2 * part + i, 256 * g + u:256 * (g + 1):2])
 
         def h_gain(q, g):
-            c, rows = place(q)
-            if (c, g) not in hp_bf:
-                hp_bf[c, g] = staged("hp_bf", [P, CHUNKS[c][1], PACK], BF16)
+            c, part = place(q)
+            if c not in hp_bf:
+                hp_bf[c] = staged_pair("hp_bf", [P, GROUPS, CHUNKS[c][1] * PACK])
             nc.vector.tensor_tensor(
-                out=hp_bf[c, g][:, rows, :].rearrange("p b (u e) -> p b u e", e=2),
+                out=hp_bf[c][:, g, :].rearrange("p (b u e) -> p b u e", u=2, e=2)[:, rows_of(part)],
                 in0=h_banks[q, g][:].bitcast(BF16).rearrange("p (u b e) -> p b u e", u=2, e=2),
-                in1=p_bf[:, g, :].rearrange("p (u e) -> p u e", e=2).unsqueeze(1).to_broadcast([P, HALF, 2, 2]),
+                in1=p_bf[:, g, :].rearrange("p (u e) -> p u e", e=2).unsqueeze(1).to_broadcast([P, QUARTER, 2, 2]),
                 op=ALU.mult,
             )
 
         def h_keep(q, g):
-            c, rows = place(q)
+            c, part = place(q)
             if (c, g) not in mid:
                 mid[c, g] = keep.tile([P, PACK, CHUNKS[c][1]], F32, name="mid_%d_%d" % (c, g))
             nc.scalar.activation(
-                out=mid[c, g][:, :, rows].rearrange("p (u e) b -> p u e b", e=2),
+                out=mid[c, g][:, :, rows_of(part)].rearrange("p (u e) b -> p u e b", e=2),
                 in_=h_banks[q, g][:].bitcast(BF16).rearrange("p (u b e) -> p u e b", u=2, e=2),
                 func=ACT.Copy, scale=1.125,
             )
 
-        def h_halve(q):
-            nc.vector.tensor_scalar(out=h_rows[q][:], in0=h_rows[q][:], scalar1=0.5, scalar2=None, op0=ALU.mult)
+        def h_halve(c):
+            nc.vector.tensor_scalar(out=h_rows[c][:], in0=h_rows[c][:], scalar1=0.5, scalar2=None, op0=ALU.mult)
 
-        def h_quantize(c, g):
-            quantize(s_codes[0][:, g, batch(c)], s_plane[0][:, g, batch(c)], hp_bf[c, g][:].rearrange("p b t -> p (b t)"))
+        def h_quantize(c):
+            quantize_state(0, c, hp_bf[c])
 
         x_banks = {}
         x_bf = {}
 
+        def keep_words(dst, bank):
+            nc.scalar.copy(out=dst, in_=bank[:].rearrange("p (u b) -> p b u", u=2))
+
+        def as_values(words):
+            return words[:].rearrange("p b u -> p (b u)").bitcast(BF16)
+
         def x_turn(q):
             words = x_rows[q][:].bitcast(F32)
-            x_banks[q] = new_bank()
-            for u in range(2):
-                for i in range(2):
-                    slot = 2 * u + i
-                    nc.tensor.transpose(x_banks[q][:, slot * P:(slot + 1) * P], words[:, i, u::2], ident[:])
+            x_banks[q] = turn_words(lambda i, u: words[:, i, u::2])
 
         def x_keep(q):
-            c, rows = place(q)
+            c, part = place(q)
             if c not in x_bf:
                 x_bf[c] = staged("x_bf", [P, CHUNKS[c][1], 2], F32)
-            nc.scalar.copy(out=x_bf[c][:, rows, :], in_=x_banks[q][:].rearrange("p (u b) -> p b u", u=2))
+            keep_words(x_bf[c][:, rows_of(part), :], x_banks[q])
 
         def x_quantize(c):
-            quantize(x_codes[:, batch(c)], x_plane[:, batch(c)], x_bf[c][:].rearrange("p b u -> p (b u)").bitcast(BF16))
+            quantize(x_codes[:, batch(c)], x_plane[:, batch(c)], as_values(x_bf[c]))
 
         z_banks = {}
-        state = {}
+        tanh_z = {}
 
         def z_matmul(stage, c, g, u):
-            cols = batch(c)
             for t in (2 * u, 2 * u + 1):
                 ch = slice(g * GROUP + t * P, g * GROUP + (t + 1) * P)
                 bank = new_bank()
@@ -303,106 +344,159 @@ def tile_antisymmetricssprk2step_x2_kernel(tc, h, x, w, win_words, win_scales, b
                 z_banks[stage, c, g, t] = z
                 nc.tensor.matmul_mx(
                     out=z, lhsT=win_codes[:, ch].bitcast(FP8X4), lhsT_scale=win_plane[:, ch],
-                    rhs=x_codes[:, cols].bitcast(FP8X4), rhs_scale=x_plane[:, cols], start=True, stop=False,
+                    rhs=x_codes[:, batch(c)].bitcast(FP8X4), rhs_scale=x_plane[:, batch(c)], start=True, stop=False,
                 )
                 for kg in range(GROUPS):
                     nc.tensor.matmul_mx(
                         out=z, lhsT=a_codes[:, kg, ch].bitcast(FP8X4), lhsT_scale=a_plane[:, kg, ch],
-                        rhs=s_codes[stage][:, kg, cols].bitcast(FP8X4), rhs_scale=s_plane[stage][:, kg, cols],
+                        rhs=s_codes[stage, c][:, kg, :].bitcast(FP8X4), rhs_scale=s_plane[stage, c][:, kg, :],
                         start=False, stop=(kg == GROUPS - 1),
                     )
 
         def z_tanh(stage, c, g, u):
-            if (stage, c, g) not in state:
-                state[stage, c, g] = work.tile([P, PACK, CHUNKS[c][1]], F32, name="tanh_z", tag="wide", bufs=5)
+            if (stage, c, g) not in tanh_z:
+                tanh_z[stage, c, g] = wide("tanh_z", CHUNKS[c][1])
             for t in (2 * u, 2 * u + 1):
                 nc.scalar.activation(
-                    out=state[stage, c, g][:, t, :], in_=z_banks[stage, c, g, t], func=ACT.Tanh, bias=b_bf[:, g, t:t + 1]
+                    out=tanh_z[stage, c, g][:, t, :], in_=z_banks[stage, c, g, t], func=ACT.Tanh, bias=b_bf[:, g, t:t + 1]
                 )
 
         up_bf = {}
 
-        def mid_update(c, g, u):
-            pair = mid[c, g][:, 2 * u:2 * u + 2, :]
+        def mid_update(c, g):
             nc.vector.scalar_tensor_tensor(
-                out=pair, in0=state[0, c, g][:, 2 * u:2 * u + 2, :], scalar=0.75, in1=pair, op0=ALU.mult, op1=ALU.add
+                out=mid[c, g][:], in0=tanh_z[0, c, g][:], scalar=0.75, in1=mid[c, g][:], op0=ALU.mult, op1=ALU.add
             )
 
         def mid_gain(c, g):
-            up_bf[c, g] = staged("up_bf", [P, CHUNKS[c][1] * PACK], BF16)
+            if c not in up_bf:
+                up_bf[c] = staged_pair("up_bf", [P, GROUPS, CHUNKS[c][1] * PACK])
             nc.vector.tensor_tensor(
-                out=up_bf[c, g][:].rearrange("p (c i t) -> p c t i", i=2, t=PACK),
-                in0=mid[c, g][:].rearrange("p t (c i) -> p c t i", i=2),
-                in1=gain_p[:, g * PACK:(g + 1) * PACK, :].unsqueeze(1).to_broadcast([P, CHUNKS[c][1] // 2, PACK, 2]),
-                op=ALU.mult,
+                out=interleaved(up_bf[c][:, g, :], 2), in0=by_slot(mid[c, g][:], 2),
+                in1=along(gain_pairs, g, CHUNKS[c][1]), op=ALU.mult,
             )
 
-        def mid_quantize(c, g):
-            quantize(s_codes[1][:, g, batch(c)], s_plane[1][:, g, batch(c)], up_bf[c, g][:])
+        def mid_quantize(c):
+            quantize_state(1, c, up_bf[c])
 
-        out_bf = {}
+        def last_update(c, g):
+            nc.vector.scalar_tensor_tensor(
+                out=tanh_z[0, c, g][:], in0=tanh_z[0, c, g][:], scalar=0.75, in1=mid[c, g][:], op0=ALU.mult, op1=ALU.add
+            )
+
+        def last_gain(c, g):
+            if c not in up_bf:
+                up_bf[c] = staged_pair("up_bf", [P, GROUPS, CHUNKS[c][1] * PACK])
+            nc.vector.tensor_tensor(
+                out=interleaved(up_bf[c][:, g, :], 2), in0=by_slot(tanh_z[0, c, g][:], 2),
+                in1=along(gain_pairs, g, CHUNKS[c][1]), op=ALU.mult,
+            )
+
+        def last_carry(c, g):
+            nc.vector.scalar_tensor_tensor(
+                out=mid[c, g][:], in0=mid[c, g][:], scalar=16.0 / 9.0, in1=tanh_z[0, c, g][:], op0=ALU.mult, op1=ALU.add
+            )
+
+        def last_sum(c, g):
+            nc.vector.tensor_tensor(out=tanh_z[1, c, g][:], in0=tanh_z[1, c, g][:], in1=mid[c, g][:], op=ALU.add)
+
+        def last_round(c, g, on_vector):
+            out_bf[c, g] = staged("out_bf", [P, CHUNKS[c][1], 2], F32)
+            dst = interleaved(as_values(out_bf[c, g]), 2)
+            if on_vector:
+                nc.vector.tensor_scalar(
+                    out=dst, in0=by_slot(tanh_z[1, c, g][:], 2), scalar1=0.25, scalar2=None, op0=ALU.mult
+                )
+            else:
+                nc.scalar.activation(out=dst, in_=by_slot(tanh_z[1, c, g][:], 2), func=ACT.Copy, scale=0.25)
+
+        def last_turn(q, g, i):
+            c, part = place(q)
+            out_banks[q, g, i] = new_bank()
+            rows = slice((2 * part + i) * P, (2 * part + i + 1) * P)
+            for t in range(PACK):
+                nc.tensor.transpose(out_banks[q, g, i][:, t * P:(t + 1) * P], tanh_z[1, c, g][:, t, rows], ident[:])
+
+        def last_keep(q, g, i):
+            c, part = place(q)
+            if (c, g) not in out_rows:
+                out_rows[c, g] = work.tile([P, CHUNKS[c][1] // P, GROUP], F32, name="out_rows", bufs=2)
+            nc.scalar.activation(
+                out=out_rows[c, g][:, 2 * part + i, :].rearrange("p (m t) -> p m t", t=PACK),
+                in_=out_banks[q, g, i][:].rearrange("p (t m) -> p m t", t=PACK),
+                func=ACT.Copy, scale=0.25,
+            )
+
+        def last_store(q, g, i):
+            c, part = place(q)
+            first = q * QUARTER + i * P
+            nc.sync.dma_start(out=out_0[first:first + P, g * GROUP:(g + 1) * GROUP], in_=out_rows[c, g][:, 2 * part + i, :])
+
         out_banks = {}
         out_rows = {}
         out_words = {}
         plane_banks = {}
+        out_bf = {}
 
         def out_turn(q, g, i):
-            c, rows = place(q)
+            c, part = place(q)
             out_banks[q, g, i] = new_bank()
-            first = rows.start + i * P
+            rows = slice((2 * part + i) * P, (2 * part + i + 1) * P)
             for t in range(PACK):
                 slot = out_banks[q, g, i][:, t * P:(t + 1) * P]
                 nc.tensor.matmul(
-                    out=slot, lhsT=mid[c, g][:, t, first:first + P], rhs=ident[:], is_transpose=True, start=True, stop=False
+                    out=slot, lhsT=mid[c, g][:, t, rows], rhs=ident[:], is_transpose=True, start=True, stop=False
                 )
                 nc.tensor.matmul(
-                    out=slot, lhsT=state[1, c, g][:, t, first:first + P], rhs=ident[:], is_transpose=True, start=False, stop=True
+                    out=slot, lhsT=tanh_z[1, c, g][:, t, rows], rhs=ident[:], is_transpose=True, start=False, stop=True
                 )
 
         def out_update(q, g, i):
-            if (q, g) not in out_rows:
-                out_rows[q, g] = work.tile([P, 2, GROUP], F32, name="out_rows", bufs=4)
+            c, part = place(q)
+            if (c, g) not in out_rows:
+                out_rows[c, g] = work.tile([P, CHUNKS[c][1] // P, GROUP], F32, name="out_rows", bufs=2)
             nc.vector.scalar_tensor_tensor(
-                out=out_rows[q, g][:, i, :].rearrange("p (m t) -> p m t", t=PACK),
+                out=out_rows[c, g][:, 2 * part + i, :].rearrange("p (m t) -> p m t", t=PACK),
                 in0=out_banks[q, g, i][:].rearrange("p (t m) -> p m t", t=PACK),
                 scalar=0.25,
-                in1=h_rows[q][:, i, g * GROUP:(g + 1) * GROUP].rearrange("p (m t) -> p m t", t=PACK),
+                in1=h_rows[c][:, 2 * part + i, g * GROUP:(g + 1) * GROUP].rearrange("p (m t) -> p m t", t=PACK),
                 op0=ALU.mult, op1=ALU.add,
             )
 
         def out_store(q, g):
+            c, part = place(q)
             nc.sync.dma_start(
-                out=out_0[q * HALF:(q + 1) * HALF, g * GROUP:(g + 1) * GROUP].rearrange("(i p) d -> p i d", p=P),
-                in_=out_rows[q, g][:],
+                out=out_0[rows_of(q), g * GROUP:(g + 1) * GROUP].rearrange("(i p) d -> p i d", p=P),
+                in_=out_rows[c, g][:, 2 * part:2 * part + 2, :],
             )
 
-        def out_round(q, g, on_vector):
-            out_words[q, g] = work.tile([P, 2, HALF, 2], BF16, name="out_words", bufs=3)
-            src = out_rows[q, g][:].rearrange("p i (m u e) -> p u (i m) e", u=2, e=2)
+        def out_round(q, g, quarters, on_vector):
+            c, part = place(q)
+            words = work.tile([P, 2, quarters * QUARTER, 2], BF16, name="out_words")
+            for k in range(quarters):
+                out_words[q + k, g] = words[:].rearrange("p u m e -> p u (m e)").bitcast(F32)[:, :, rows_of(k)]
+            src = out_rows[c, g][:, 2 * part:2 * (part + quarters), :].rearrange("p i (m u e) -> p u (i m) e", u=2, e=2)
             if on_vector:
-                nc.vector.tensor_copy(out=out_words[q, g][:], in_=src)
+                nc.vector.tensor_copy(out=words[:], in_=src)
             else:
-                nc.scalar.copy(out=out_words[q, g][:], in_=src)
+                nc.scalar.copy(out=words[:], in_=src)
 
         def plane_turn(q, g):
-            words = out_words[q, g][:].rearrange("p u m e -> p (u m e)").bitcast(F32)
-            plane_banks[q, g] = new_bank()
-            for slot in range(4):
-                cols = slice(slot * P, (slot + 1) * P)
-                nc.tensor.transpose(plane_banks[q, g][:, cols], words[:, cols], ident[:])
+            plane_banks[q, g] = turn_words(lambda i, u: out_words[q, g][:, u, i * P:(i + 1) * P])
 
         def plane_keep(q, g):
-            c, rows = place(q)
+            c, part = place(q)
             if (c, g) not in out_bf:
                 out_bf[c, g] = staged("out_bf", [P, CHUNKS[c][1], 2], F32)
-            nc.scalar.copy(out=out_bf[c, g][:, rows, :], in_=plane_banks[q, g][:].rearrange("p (u b) -> p b u", u=2))
+            keep_words(out_bf[c, g][:, rows_of(part), :], plane_banks[q, g])
 
-        def out_planes(c, g):
-            codes = work.tile([P, CHUNKS[c][1]], U32, name="out_codes", align_bytes=64)
-            quantize(codes[:], out_plane[:, g, batch(c)], out_bf[c, g][:].rearrange("p b u -> p (b u)").bitcast(BF16))
-            nc.sync.dma_start(
-                out=out_1[g].rearrange("p m t -> p (m t)").bitcast(I32)[:, batch(c)], in_=codes[:].bitcast(I32)
-            )
+        def out_planes(q, g, quarters):
+            c, part = place(q)
+            cols = slice(q * QUARTER, (q + quarters) * QUARTER)
+            codes = work.tile([P, quarters * QUARTER], U32, name="out_codes", align_bytes=64)
+            values = out_bf[c, g][:, part * QUARTER:(part + quarters) * QUARTER, :]
+            quantize(codes[:], out_plane[:, g, cols], values.rearrange("p b u -> p (b u)").bitcast(BF16))
+            nc.sync.dma_start(out=out_1[g].rearrange("p m t -> p (m t)").bitcast(I32)[:, cols], in_=codes[:].bitcast(I32))
 
         def out_scales(g):
             for quad in range(4):
@@ -412,228 +506,214 @@ def tile_antisymmetricssprk2step_x2_kernel(tc, h, x, w, win_words, win_scales, b
                 )
 
         ctx.enter_context(tc.manual_schedule())
-        a_direct(0, 0, 0, False)
         a_turn(0, 0, 0)
+        diff_subtract(0, 0, 0)
         a_turn(0, 0, 1)
-        a_turned(0, 0, 0)
-        a_turn(1, 0, 0)
-        a_turned(0, 0, 1)
-        a_direct(0, 0, 1, True)
-        diff_subtract(0)
-        a_turn(1, 0, 1)
-        diff_subtract(1)
-        h_turn(0, 1)
-        diff_scale(0)
-        diff_scale(1)
-        x_turn(0)
-        win_move_scales()
-        diff_turn(3)
-        diff_turn(0)
-        x_keep(0)
-        h_gain(0, 1)
-        diff_turn(2)
-        diff_turn(1)
-        win_move_codes()
-        a_subtract(0, 0)
-        diff_turned(0)
-        diff_turned(2)
-        a_interleave(1, 0)
-        h_keep(0, 1)
-        diff_turned(1)
-        h_turn(1, 1)
-        h_quantize(0, 1)
-        h_gain(1, 1)
+        diff_subtract(0, 0, 1)
         h_turn(0, 0)
+        h_turn(0, 1)
         h_gain(0, 0)
-        diff_turned(3)
+        h_gain(0, 1)
+        diff_scale(0, 0, 0)
+        diff_scale(0, 0, 1)
+        a_turn(1, 0, 0)
+        h_halve(0)
+        a_turn(1, 0, 1)
+        diff_subtract(1, 0, 0)
+        h_keep(0, 0)
+        x_turn(0)
+        h_quantize(0)
+        h_keep(0, 1)
+        diff_subtract(1, 0, 1)
+        diff_scale(1, 0, 0)
+        diff_scale(1, 0, 1)
+        a_interleave(0, 0)
+        win_move_scales()
         a_quantize(0, 0)
-        h_turn(2, 0)
-        h_quantize(0, 0)
+        x_keep(0)
         h_turn(1, 0)
-        x_quantize(0)
-        a_interleave(0, 1)
-        a_quantize(1, 0)
-        h_gain(1, 0)
+        a_direct(1, 1, 0)
+        win_move_codes()
+        diff_turn(0)
         a_turn(1, 1, 0)
-        a_direct(1, 1, 0, False)
-        a_direct(1, 1, 1, False)
+        h_turn(1, 1)
+        h_turn(2, 1)
+        a_interleave(1, 0)
+        h_gain(1, 0)
+        a_quantize(1, 0)
+        diff_turned(0)
+        h_gain(1, 1)
+        diff_turn(1)
+        diff_turn(2)
+        diff_turn(3)
+        x_quantize(0)
+        diff_turned(1)
+        diff_turned(2)
+        diff_turned(3)
+        a_direct(1, 1, 1)
+        h_turn(2, 0)
         a_turn(1, 1, 1)
+        h_gain(2, 0)
+        a_interleave(0, 1)
+        x_turn(3)
+        h_gain(2, 1)
+        x_keep(3)
+        x_turn(1)
         a_quantize(0, 1)
+        x_quantize(2)
+        h_quantize(1)
         a_turned(1, 1, 0)
         a_turned(1, 1, 1)
-        h_keep(0, 0)
-        a_subtract(1, 1)
-        h_gain(2, 0)
-        z_matmul(0, 0, 0, 0)
-        z_tanh(0, 0, 0, 0)
-        mid_update(0, 0, 0)
-        h_keep(1, 0)
-        x_turn(1)
-        h_turn(2, 1)
-        h_turn(3, 0)
         x_turn(2)
+        a_subtract(1, 1)
         x_keep(1)
         x_keep(2)
-        x_turn(3)
-        h_turn(3, 1)
-        x_keep(3)
-        z_matmul(0, 0, 0, 1)
-        h_gain(2, 1)
-        a_quantize(1, 1)
-        z_tanh(0, 0, 0, 1)
         x_quantize(1)
-        z_matmul(0, 0, 1, 0)
-        z_tanh(0, 0, 1, 0)
-        z_matmul(0, 0, 1, 1)
-        z_tanh(0, 0, 1, 1)
-        h_quantize(1, 0)
-        h_quantize(1, 1)
-        z_matmul(0, 1, 1, 0)
+        z_matmul(0, 0, 0, 0)
+        h_turn(3, 0)
+        z_tanh(0, 0, 0, 0)
+        h_turn(3, 1)
+        a_quantize(1, 1)
         h_gain(3, 0)
-        mid_update(0, 0, 1)
-        h_keep(2, 0)
-        z_tanh(0, 1, 1, 0)
         h_gain(3, 1)
-        mid_gain(0, 0)
-        mid_update(0, 1, 1)
+        h_keep(1, 1)
+        z_matmul(0, 0, 0, 1)
+        z_tanh(0, 0, 0, 1)
+        mid_update(0, 0)
+        h_keep(1, 0)
+        h_quantize(2)
+        z_matmul(0, 0, 1, 0)
+        z_matmul(0, 0, 1, 1)
+        z_tanh(0, 0, 1, 0)
+        z_tanh(0, 0, 1, 1)
+        h_keep(2, 0)
         z_matmul(0, 1, 0, 0)
+        mid_update(0, 1)
         z_matmul(0, 1, 0, 1)
         z_tanh(0, 1, 0, 0)
-        x_quantize(2)
-        mid_update(0, 1, 0)
-        h_quantize(2, 0)
-        mid_gain(0, 1)
-        mid_quantize(0, 0)
-        z_matmul(0, 1, 1, 1)
-        mid_quantize(0, 1)
-        h_keep(1, 1)
-        h_keep(2, 1)
-        h_quantize(2, 1)
         z_tanh(0, 1, 0, 1)
-        mid_update(1, 0, 0)
+        h_keep(2, 1)
+        z_matmul(0, 2, 1, 0)
+        z_tanh(0, 2, 1, 0)
+        z_matmul(0, 1, 1, 0)
+        mid_gain(0, 0)
+        mid_gain(0, 1)
+        z_matmul(0, 2, 0, 1)
+        z_matmul(0, 1, 1, 1)
+        z_tanh(0, 1, 1, 0)
+        z_tanh(0, 1, 1, 1)
+        mid_update(1, 0)
+        z_matmul(0, 2, 0, 0)
+        z_tanh(0, 2, 0, 0)
+        z_tanh(0, 2, 0, 1)
+        mid_quantize(0)
+        z_matmul(1, 0, 0, 0)
+        z_matmul(0, 2, 1, 1)
+        z_tanh(1, 0, 0, 0)
+        mid_gain(1, 0)
+        z_matmul(1, 0, 0, 1)
+        z_tanh(1, 0, 0, 1)
         z_matmul(1, 0, 1, 0)
         z_tanh(1, 0, 1, 0)
-        mid_update(1, 1, 0)
-        z_matmul(0, 2, 0, 0)
-        z_tanh(0, 1, 1, 1)
-        z_tanh(0, 2, 0, 0)
-        z_matmul(0, 2, 0, 1)
-        z_tanh(0, 2, 0, 1)
         z_matmul(1, 0, 1, 1)
-        z_tanh(1, 0, 1, 1)
-        z_matmul(0, 2, 1, 1)
-        mid_update(1, 0, 1)
-        z_matmul(1, 0, 0, 0)
-        mid_update(1, 1, 1)
-        mid_gain(1, 0)
-        z_tanh(1, 0, 0, 0)
-        mid_gain(1, 1)
-        z_matmul(1, 0, 0, 1)
-        mid_quantize(1, 0)
-        z_tanh(1, 0, 0, 1)
-        mid_quantize(1, 1)
-        h_halve(0)
-        z_matmul(0, 2, 1, 0)
         out_turn(0, 0, 0)
-        out_update(0, 0, 0)
-        out_turn(0, 0, 1)
-        out_update(0, 0, 1)
-        z_tanh(0, 2, 1, 0)
-        z_tanh(0, 2, 1, 1)
+        mid_update(1, 1)
+        mid_gain(1, 1)
+        mid_quantize(1)
+        z_tanh(1, 0, 1, 1)
+        out_turn(0, 1, 1)
         out_turn(0, 1, 0)
         out_update(0, 1, 0)
-        out_turn(0, 1, 1)
-        h_keep(3, 0)
-        mid_update(2, 0, 0)
-        h_keep(3, 1)
-        mid_update(2, 0, 1)
-        z_matmul(1, 1, 1, 1)
-        out_update(0, 1, 1)
-        out_store(0, 1)
-        mid_gain(2, 0)
-        mid_quantize(2, 0)
+        out_turn(0, 0, 1)
+        z_tanh(0, 2, 1, 1)
+        out_update(0, 0, 0)
+        out_update(0, 0, 1)
         z_matmul(1, 1, 1, 0)
-        mid_update(2, 1, 1)
-        mid_update(2, 1, 0)
-        mid_gain(2, 1)
+        h_keep(3, 0)
+        h_keep(3, 1)
+        z_matmul(1, 1, 0, 0)
+        last_update(2, 1)
+        out_update(0, 1, 1)
+        z_matmul(1, 1, 1, 1)
+        out_round(0, 0, 1, False)
+        z_matmul(1, 1, 0, 1)
         z_tanh(1, 1, 1, 0)
         z_tanh(1, 1, 1, 1)
-        out_round(0, 1, False)
-        z_matmul(1, 1, 0, 1)
-        out_round(0, 0, False)
-        z_matmul(1, 1, 0, 0)
-        z_tanh(1, 1, 0, 0)
-        out_turn(1, 1, 1)
-        plane_turn(0, 1)
-        plane_keep(0, 1)
-        mid_quantize(2, 1)
-        z_tanh(1, 1, 0, 1)
-        h_halve(1)
-        out_turn(1, 1, 0)
-        out_update(1, 1, 0)
-        h_halve(2)
-        out_update(1, 1, 1)
         out_store(0, 0)
+        out_turn(1, 1, 0)
+        out_turn(1, 1, 1)
+        last_update(2, 0)
+        out_store(0, 1)
+        h_halve(1)
+        last_gain(2, 0)
+        last_gain(2, 1)
         out_turn(2, 1, 1)
-        z_matmul(1, 2, 1, 0)
-        z_tanh(1, 2, 1, 0)
-        z_matmul(1, 2, 1, 1)
-        out_planes(0, 1)
+        out_round(0, 1, 1, False)
+        z_tanh(1, 1, 0, 0)
+        out_update(1, 1, 0)
+        out_update(1, 1, 1)
         plane_turn(0, 0)
-        z_tanh(1, 2, 1, 1)
-        out_round(1, 1, False)
+        out_update(2, 1, 1)
         out_turn(2, 1, 0)
         out_update(2, 1, 0)
-        out_store(1, 1)
-        out_update(2, 1, 1)
-        out_store(2, 1)
-        out_turn(1, 0, 0)
-        plane_keep(0, 0)
-        out_planes(0, 0)
-        out_turn(1, 0, 1)
-        out_round(2, 1, False)
-        out_update(1, 0, 0)
+        mid_quantize(2)
+        plane_turn(0, 1)
+        z_tanh(1, 1, 0, 1)
         out_turn(2, 0, 0)
+        out_turn(1, 0, 1)
+        plane_keep(0, 0)
+        last_carry(2, 1)
+        out_planes(0, 0, 1)
+        out_turn(1, 0, 0)
+        out_update(1, 0, 0)
         out_update(1, 0, 1)
-        out_round(1, 0, False)
-        out_turn(3, 1, 1)
-        h_halve(3)
-        plane_turn(1, 1)
-        out_turn(3, 1, 0)
-        out_update(3, 1, 0)
-        out_update(3, 1, 1)
-        plane_keep(1, 1)
+        out_store(2, 1)
+        plane_keep(0, 1)
+        z_matmul(1, 2, 1, 0)
+        out_planes(0, 1, 1)
+        out_round(1, 1, 2, False)
+        z_matmul(1, 2, 1, 1)
+        z_tanh(1, 2, 1, 0)
+        z_tanh(1, 2, 1, 1)
         plane_turn(2, 1)
-        plane_keep(2, 1)
-        z_matmul(1, 2, 0, 1)
-        out_store(1, 0)
-        out_store(3, 1)
+        plane_turn(1, 1)
+        out_turn(2, 0, 1)
+        out_update(2, 0, 0)
+        plane_keep(1, 1)
         z_matmul(1, 2, 0, 0)
+        z_matmul(1, 2, 0, 1)
+        plane_keep(2, 1)
         z_tanh(1, 2, 0, 0)
         z_tanh(1, 2, 0, 1)
-        out_update(2, 0, 0)
-        out_turn(2, 0, 1)
-        out_round(3, 1, True)
-        plane_turn(3, 1)
-        out_turn(3, 0, 0)
-        out_planes(1, 1)
-        plane_keep(3, 1)
+        last_sum(2, 1)
+        last_turn(3, 1, 0)
         out_update(2, 0, 1)
-        out_round(2, 0, False)
-        out_update(3, 0, 0)
-        out_planes(2, 1)
-        out_turn(3, 0, 1)
+        last_turn(3, 1, 1)
+        out_store(1, 1)
+        out_round(1, 0, 2, False)
+        out_store(1, 0)
+        last_round(2, 1, True)
+        out_store(2, 0)
+        out_planes(1, 1, 2)
+        out_planes(3, 1, 1)
         out_scales(1)
+        last_keep(3, 1, 0)
+        last_store(3, 1, 0)
+        last_keep(3, 1, 1)
+        last_store(3, 1, 1)
         plane_turn(1, 0)
         plane_keep(1, 0)
-        out_update(3, 0, 1)
-        out_round(3, 0, False)
-        out_store(2, 0)
         plane_turn(2, 0)
+        last_carry(2, 0)
+        last_sum(2, 0)
+        last_turn(3, 0, 0)
+        last_round(2, 0, True)
         plane_keep(2, 0)
-        out_store(3, 0)
-        out_planes(1, 0)
-        plane_turn(3, 0)
-        plane_keep(3, 0)
-        out_planes(2, 0)
+        out_planes(3, 0, 1)
+        last_keep(3, 0, 0)
+        last_turn(3, 0, 1)
+        last_store(3, 0, 0)
+        last_keep(3, 0, 1)
+        out_planes(1, 0, 2)
+        last_store(3, 0, 1)
         out_scales(0)

@@ -20,7 +20,7 @@ PACK = 4
 GROUP = P * PACK
 GROUPS = D // GROUP
 QUARTER = 256
-CHUNKS = [(0, 256), (256, 512), (768, 256)]
+CHUNKS = [(0, 512), (512, 256), (768, 256)]
 
 
 def tile_antisymmetricssprk2step_x2_kernel(tc, h, x, w, win_words, win_scales, b, p, r, out_0, out_1, out_2):
@@ -58,8 +58,6 @@ def tile_antisymmetricssprk2step_x2_kernel(tc, h, x, w, win_words, win_scales, b
 
         ident = keep.tile([P, P], F32, name="ident")
         make_identity(nc, ident[:])
-        warm = keep.tile([P, 1], F32, name="warm")
-        nc.scalar.activation(out=warm[:], in_=ident[:, 0:1], func=ACT.Tanh)
 
         w_quad = {}
         h_rows = {}
@@ -82,7 +80,7 @@ def tile_antisymmetricssprk2step_x2_kernel(tc, h, x, w, win_words, win_scales, b
 
         def load_x(q):
             x_rows[q] = keep.tile([P, 2, X], BF16, name="x_%d" % q)
-            nc.sync.dma_start(out=x_rows[q][:], in_=x[rows_of(q), :].rearrange("(i p) k -> p i k", p=P))
+            nc.sync.dma_start(out=x_rows[q][:], in_=x[rows_of(q), :].rearrange("(p i) k -> p i k", p=P))
 
         def load_vector(engine, vec, name):
             loaded = keep.tile([P, GROUPS, PACK], BF16, name=name)
@@ -149,8 +147,8 @@ def tile_antisymmetricssprk2step_x2_kernel(tc, h, x, w, win_words, win_scales, b
 
         def win_move_codes():
             nc.vector.tensor_copy(
-                out=win_codes[:].rearrange("p (g t m) -> p g t m", g=GROUPS, t=PACK),
-                in_=win_raw[:].rearrange("p (g m t) -> p g t m", g=GROUPS, t=PACK),
+                out=win_codes[:].rearrange("p (g t c i) -> p g c t i", g=GROUPS, t=PACK, i=4),
+                in_=win_raw[:].rearrange("p (g c i t) -> p g c t i", g=GROUPS, t=PACK, i=4),
             )
 
         def win_move_scales():
@@ -231,6 +229,17 @@ def tile_antisymmetricssprk2step_x2_kernel(tc, h, x, w, win_words, win_scales, b
                 in1=w_banks[g, gc, u][:].bitcast(BF16).rearrange("p (t m e) -> p e t m", t=PACK, e=2),
                 op=ALU.subtract,
             )
+
+        def a_finish(u):
+            if (0, 0) not in scaled:
+                scaled[0, 0] = staged("scaled", [P, PACK, GROUP], BF16)
+            for e in range(2):
+                j = 2 * u + e
+                nc.vector.scalar_tensor_tensor(
+                    out=scaled[0, 0][:, j, :],
+                    in0=w_banks[0, 0, u][:].bitcast(BF16).rearrange("p (c e) -> p c e", e=2)[:, :, e],
+                    scalar=minus_r[:, j:j + 1], in1=rw[0, 0][:, j, :], op0=ALU.mult, op1=ALU.add,
+                )
 
         def diff_gain(g, gc):
             a_bf[g, gc] = staged("a_bf", [P, GROUP * PACK], BF16)
@@ -328,7 +337,10 @@ def tile_antisymmetricssprk2step_x2_kernel(tc, h, x, w, win_words, win_scales, b
             c, part = place(q)
             if c not in x_bf:
                 x_bf[c] = staged("x_bf", [P, CHUNKS[c][1], 2], F32)
-            keep_words(x_bf[c][:, rows_of(part), :], x_banks[q])
+            nc.scalar.copy(
+                out=x_bf[c][:, rows_of(part), :].rearrange("p (b i) u -> p b i u", i=2),
+                in_=x_banks[q][:].rearrange("p (u i b) -> p b i u", u=2, i=2),
+            )
 
         def x_quantize(c):
             quantize(x_codes[:, batch(c)], x_plane[:, batch(c)], as_values(x_bf[c]))
@@ -506,214 +518,215 @@ def tile_antisymmetricssprk2step_x2_kernel(tc, h, x, w, win_words, win_scales, b
                 )
 
         ctx.enter_context(tc.manual_schedule())
+        a_direct(0, 0, 0)
         a_turn(0, 0, 0)
-        diff_subtract(0, 0, 0)
+        a_finish(0)
         a_turn(0, 0, 1)
-        diff_subtract(0, 0, 1)
+        a_direct(0, 0, 1)
+        a_finish(1)
         h_turn(0, 0)
-        h_turn(0, 1)
         h_gain(0, 0)
-        h_gain(0, 1)
-        diff_scale(0, 0, 0)
-        diff_scale(0, 0, 1)
-        a_turn(1, 0, 0)
-        h_halve(0)
-        a_turn(1, 0, 1)
-        diff_subtract(1, 0, 0)
         h_keep(0, 0)
-        x_turn(0)
-        h_quantize(0)
+        h_turn(0, 1)
+        a_turn(1, 0, 0)
+        a_turn(1, 0, 1)
         h_keep(0, 1)
+        x_turn(0)
+        a_interleave(0, 0)
+        diff_subtract(1, 0, 0)
         diff_subtract(1, 0, 1)
+        h_turn(1, 0)
+        win_move_scales()
         diff_scale(1, 0, 0)
         diff_scale(1, 0, 1)
-        a_interleave(0, 0)
-        win_move_scales()
-        a_quantize(0, 0)
-        x_keep(0)
-        h_turn(1, 0)
-        a_direct(1, 1, 0)
-        win_move_codes()
-        diff_turn(0)
-        a_turn(1, 1, 0)
+        h_gain(0, 1)
         h_turn(1, 1)
-        h_turn(2, 1)
-        a_interleave(1, 0)
         h_gain(1, 0)
-        a_quantize(1, 0)
-        diff_turned(0)
-        h_gain(1, 1)
-        diff_turn(1)
         diff_turn(2)
+        a_direct(1, 1, 0)
+        x_keep(0)
+        h_gain(1, 1)
+        x_turn(1)
+        diff_turn(0)
         diff_turn(3)
-        x_quantize(0)
-        diff_turned(1)
-        diff_turned(2)
+        x_keep(1)
+        diff_turned(0)
         diff_turned(3)
-        a_direct(1, 1, 1)
-        h_turn(2, 0)
+        diff_turned(2)
+        a_interleave(1, 0)
+        a_turn(1, 1, 0)
+        diff_turn(1)
+        diff_turned(1)
+        a_turned(1, 1, 0)
         a_turn(1, 1, 1)
+        h_quantize(0)
+        x_quantize(0)
+        h_turn(2, 0)
+        a_quantize(1, 0)
+        h_turn(2, 1)
+        a_turned(1, 1, 1)
+        win_move_codes()
+        a_direct(1, 1, 1)
+        a_quantize(0, 0)
+        h_keep(1, 0)
+        z_matmul(0, 0, 0, 0)
         h_gain(2, 0)
         a_interleave(0, 1)
-        x_turn(3)
         h_gain(2, 1)
-        x_keep(3)
-        x_turn(1)
         a_quantize(0, 1)
-        x_quantize(2)
         h_quantize(1)
-        a_turned(1, 1, 0)
-        a_turned(1, 1, 1)
+        z_tanh(0, 0, 0, 0)
         x_turn(2)
         a_subtract(1, 1)
-        x_keep(1)
-        x_keep(2)
-        x_quantize(1)
-        z_matmul(0, 0, 0, 0)
         h_turn(3, 0)
-        z_tanh(0, 0, 0, 0)
-        h_turn(3, 1)
-        a_quantize(1, 1)
         h_gain(3, 0)
+        h_turn(3, 1)
         h_gain(3, 1)
         h_keep(1, 1)
+        a_quantize(1, 1)
+        h_quantize(2)
         z_matmul(0, 0, 0, 1)
         z_tanh(0, 0, 0, 1)
         mid_update(0, 0)
-        h_keep(1, 0)
-        h_quantize(2)
-        z_matmul(0, 0, 1, 0)
-        z_matmul(0, 0, 1, 1)
-        z_tanh(0, 0, 1, 0)
-        z_tanh(0, 0, 1, 1)
-        h_keep(2, 0)
-        z_matmul(0, 1, 0, 0)
-        mid_update(0, 1)
-        z_matmul(0, 1, 0, 1)
-        z_tanh(0, 1, 0, 0)
-        z_tanh(0, 1, 0, 1)
         h_keep(2, 1)
+        x_keep(2)
+        x_quantize(1)
+        z_matmul(0, 0, 1, 0)
+        z_tanh(0, 0, 1, 0)
+        z_matmul(0, 0, 1, 1)
+        z_tanh(0, 0, 1, 1)
+        mid_gain(0, 0)
+        mid_update(0, 1)
+        x_turn(3)
+        h_keep(2, 0)
+        x_keep(3)
+        x_quantize(2)
+        z_matmul(0, 1, 1, 1)
+        z_matmul(0, 1, 1, 0)
+        z_tanh(0, 1, 1, 0)
+        z_matmul(0, 1, 0, 1)
+        mid_gain(0, 1)
+        z_matmul(0, 1, 0, 0)
+        mid_quantize(0)
+        z_tanh(0, 1, 1, 1)
+        last_update(1, 1)
+        z_tanh(0, 1, 0, 0)
+        z_matmul(0, 2, 0, 0)
+        h_keep(3, 1)
+        z_tanh(0, 2, 0, 0)
+        z_tanh(0, 1, 0, 1)
+        mid_update(1, 0)
+        h_halve(1)
         z_matmul(0, 2, 1, 0)
         z_tanh(0, 2, 1, 0)
-        z_matmul(0, 1, 1, 0)
-        mid_gain(0, 0)
-        mid_gain(0, 1)
         z_matmul(0, 2, 0, 1)
-        z_matmul(0, 1, 1, 1)
-        z_tanh(0, 1, 1, 0)
-        z_tanh(0, 1, 1, 1)
-        mid_update(1, 0)
-        z_matmul(0, 2, 0, 0)
-        z_tanh(0, 2, 0, 0)
-        z_tanh(0, 2, 0, 1)
-        mid_quantize(0)
-        z_matmul(1, 0, 0, 0)
         z_matmul(0, 2, 1, 1)
-        z_tanh(1, 0, 0, 0)
         mid_gain(1, 0)
-        z_matmul(1, 0, 0, 1)
-        z_tanh(1, 0, 0, 1)
+        last_gain(1, 1)
+        z_matmul(1, 0, 1, 1)
+        last_carry(1, 1)
+        z_tanh(0, 2, 0, 1)
+        h_keep(3, 0)
         z_matmul(1, 0, 1, 0)
         z_tanh(1, 0, 1, 0)
-        z_matmul(1, 0, 1, 1)
-        out_turn(0, 0, 0)
-        mid_update(1, 1)
-        mid_gain(1, 1)
-        mid_quantize(1)
+        z_matmul(1, 0, 0, 0)
         z_tanh(1, 0, 1, 1)
         out_turn(0, 1, 1)
-        out_turn(0, 1, 0)
-        out_update(0, 1, 0)
-        out_turn(0, 0, 1)
-        z_tanh(0, 2, 1, 1)
-        out_update(0, 0, 0)
-        out_update(0, 0, 1)
-        z_matmul(1, 1, 1, 0)
-        h_keep(3, 0)
-        h_keep(3, 1)
-        z_matmul(1, 1, 0, 0)
-        last_update(2, 1)
-        out_update(0, 1, 1)
-        z_matmul(1, 1, 1, 1)
-        out_round(0, 0, 1, False)
-        z_matmul(1, 1, 0, 1)
-        z_tanh(1, 1, 1, 0)
-        z_tanh(1, 1, 1, 1)
-        out_store(0, 0)
-        out_turn(1, 1, 0)
         out_turn(1, 1, 1)
-        last_update(2, 0)
-        out_store(0, 1)
-        h_halve(1)
-        last_gain(2, 0)
-        last_gain(2, 1)
-        out_turn(2, 1, 1)
-        out_round(0, 1, 1, False)
-        z_tanh(1, 1, 0, 0)
+        z_tanh(1, 0, 0, 0)
+        out_turn(0, 1, 0)
+        h_halve(0)
+        mid_quantize(1)
+        z_tanh(0, 2, 1, 1)
+        out_update(0, 1, 0)
+        out_update(0, 1, 1)
+        out_turn(1, 1, 0)
         out_update(1, 1, 0)
+        z_matmul(1, 1, 0, 0)
+        z_tanh(1, 1, 0, 0)
         out_update(1, 1, 1)
-        plane_turn(0, 0)
-        out_update(2, 1, 1)
-        out_turn(2, 1, 0)
-        out_update(2, 1, 0)
-        mid_quantize(2)
-        plane_turn(0, 1)
+        out_store(0, 1)
+        last_update(2, 1)
+        z_matmul(1, 1, 0, 1)
+        last_update(2, 0)
+        z_matmul(1, 1, 1, 0)
         z_tanh(1, 1, 0, 1)
         out_turn(2, 0, 0)
-        out_turn(1, 0, 1)
-        plane_keep(0, 0)
-        last_carry(2, 1)
-        out_planes(0, 0, 1)
-        out_turn(1, 0, 0)
-        out_update(1, 0, 0)
-        out_update(1, 0, 1)
-        out_store(2, 1)
-        plane_keep(0, 1)
-        z_matmul(1, 2, 1, 0)
-        out_planes(0, 1, 1)
-        out_round(1, 1, 2, False)
-        z_matmul(1, 2, 1, 1)
-        z_tanh(1, 2, 1, 0)
-        z_tanh(1, 2, 1, 1)
-        plane_turn(2, 1)
-        plane_turn(1, 1)
-        out_turn(2, 0, 1)
         out_update(2, 0, 0)
+        out_turn(2, 0, 1)
+        out_update(2, 0, 1)
+        z_matmul(1, 1, 1, 1)
+        out_store(1, 1)
+        out_round(0, 1, 2, False)
+        last_gain(2, 0)
+        out_store(2, 0)
+        z_tanh(1, 1, 1, 0)
+        z_tanh(1, 1, 1, 1)
+        out_round(2, 0, 1, False)
+        z_matmul(1, 0, 0, 1)
+        z_tanh(1, 0, 0, 1)
+        plane_turn(1, 1)
+        last_sum(1, 1)
+        plane_turn(0, 1)
+        plane_turn(2, 0)
+        last_turn(2, 1, 0)
+        plane_keep(2, 0)
+        last_keep(2, 1, 0)
+        plane_keep(0, 1)
+        last_store(2, 1, 0)
+        last_gain(2, 1)
+        last_carry(2, 1)
+        out_turn(0, 0, 0)
+        out_turn(1, 0, 0)
+        out_planes(2, 0, 1)
+        last_turn(2, 1, 1)
+        mid_quantize(2)
+        out_update(0, 0, 0)
+        out_update(1, 0, 0)
+        out_turn(0, 0, 1)
+        out_turn(1, 0, 1)
+        out_update(1, 0, 1)
+        out_store(1, 0)
+        last_round(1, 1, False)
         plane_keep(1, 1)
+        last_keep(2, 1, 1)
+        z_matmul(1, 2, 1, 0)
+        out_planes(2, 1, 1)
+        z_tanh(1, 2, 1, 0)
+        last_store(2, 1, 1)
+        z_matmul(1, 2, 1, 1)
+        z_tanh(1, 2, 1, 1)
         z_matmul(1, 2, 0, 0)
+        out_update(0, 0, 1)
+        out_store(0, 0)
         z_matmul(1, 2, 0, 1)
-        plane_keep(2, 1)
+        last_carry(2, 0)
+        out_round(0, 0, 2, False)
         z_tanh(1, 2, 0, 0)
         z_tanh(1, 2, 0, 1)
         last_sum(2, 1)
         last_turn(3, 1, 0)
-        out_update(2, 0, 1)
-        last_turn(3, 1, 1)
-        out_store(1, 1)
-        out_round(1, 0, 2, False)
-        out_store(1, 0)
-        last_round(2, 1, True)
-        out_store(2, 0)
-        out_planes(1, 1, 2)
-        out_planes(3, 1, 1)
-        out_scales(1)
         last_keep(3, 1, 0)
-        last_store(3, 1, 0)
+        last_turn(3, 1, 1)
+        out_planes(0, 1, 2)
+        last_round(2, 1, True)
+        out_planes(3, 1, 1)
+        last_sum(2, 0)
         last_keep(3, 1, 1)
+        out_scales(1)
         last_store(3, 1, 1)
         plane_turn(1, 0)
+        plane_turn(0, 0)
+        plane_keep(0, 0)
         plane_keep(1, 0)
-        plane_turn(2, 0)
-        last_carry(2, 0)
-        last_sum(2, 0)
-        last_turn(3, 0, 0)
         last_round(2, 0, True)
-        plane_keep(2, 0)
+        last_store(3, 1, 0)
+        last_turn(3, 0, 0)
         out_planes(3, 0, 1)
         last_keep(3, 0, 0)
-        last_turn(3, 0, 1)
         last_store(3, 0, 0)
+        last_turn(3, 0, 1)
         last_keep(3, 0, 1)
-        out_planes(1, 0, 2)
         last_store(3, 0, 1)
+        out_planes(0, 0, 2)
         out_scales(0)

@@ -19,8 +19,13 @@ P = 128
 PACK = 4
 GROUP = P * PACK
 GROUPS = D // GROUP
+GROUP_WORDS = GROUP // 2
+BANK = 512
 QUARTER = 256
 CHUNKS = [(0, 512), (512, 256), (768, 256)]
+STAGED_BUFS = 5
+WIDE_BUFS = 5
+ON_VECTOR, ON_SCALAR = True, False
 
 
 def tile_antisymmetricssprk2step_x2_kernel(tc, h, x, w, win_words, win_scales, b, p, r, out_0, out_1, out_2):
@@ -31,16 +36,16 @@ def tile_antisymmetricssprk2step_x2_kernel(tc, h, x, w, win_words, win_scales, b
         psum = ctx.enter_context(tc.psum_pool(name="psum", bufs=8))
 
         def new_bank():
-            return psum.tile([P, 512], F32, name="bank")
+            return psum.tile([P, BANK], F32, name="bank")
 
         def staged(name, shape, dtype):
-            return work.tile(shape, dtype, name=name, tag="staged", bufs=5, align_bytes=64)
+            return work.tile(shape, dtype, name=name, tag="staged", bufs=STAGED_BUFS, align_bytes=64)
 
         def staged_pair(name, shape):
             return work.tile(shape, BF16, name=name, tag="staged_pair", bufs=2, align_bytes=64)
 
         def wide(name, width):
-            return work.tile([P, PACK, width], F32, name=name, tag="wide", bufs=5)
+            return work.tile([P, PACK, width], F32, name=name, tag="wide", bufs=WIDE_BUFS)
 
         def quantize(codes, scales, values):
             nc.vector.quantize_mx(out=codes.bitcast(FP8X4), scales=scales, in_=values)
@@ -119,19 +124,16 @@ def tile_antisymmetricssprk2step_x2_kernel(tc, h, x, w, win_words, win_scales, b
         load_h(3)
         load_x(3)
 
-        def doubled(vec_bf, factor, name):
-            pairs = keep.tile([P, GROUPS * PACK, 2], F32, name=name)
-            nc.vector.tensor_scalar(
-                out=pairs[:],
-                in0=vec_bf[:].rearrange("p g t -> p (g t)").unsqueeze(2).to_broadcast([P, GROUPS * PACK, 2]),
-                scalar1=factor, scalar2=None, op0=ALU.mult,
-            )
-            return pairs
-
-        r_pairs = doubled(r_bf, 1.0, "r_pairs")
+        r_f32 = keep.tile([P, GROUPS, PACK], F32, name="r_f32")
+        nc.vector.tensor_copy(out=r_f32[:], in_=r_bf[:])
         minus_r = keep.tile([P, PACK], F32, name="minus_r")
         nc.vector.tensor_scalar(out=minus_r[:], in0=r_bf[:, 0, :], scalar1=-1.0, scalar2=None, op0=ALU.mult)
-        gain_pairs = doubled(p_bf, 2.0 / 3.0, "gain_pairs")
+        gain_pairs = keep.tile([P, GROUPS * PACK, 2], F32, name="gain_pairs")
+        nc.vector.tensor_scalar(
+            out=gain_pairs[:],
+            in0=p_bf[:].rearrange("p g t -> p (g t)").unsqueeze(2).to_broadcast([P, GROUPS * PACK, 2]),
+            scalar1=2.0 / 3.0, scalar2=None, op0=ALU.mult,
+        )
 
         def interleaved(tile_ap, run):
             return tile_ap.rearrange("p (c i t) -> p c t i", i=run, t=PACK)
@@ -139,8 +141,8 @@ def tile_antisymmetricssprk2step_x2_kernel(tc, h, x, w, win_words, win_scales, b
         def by_slot(tile_ap, run):
             return tile_ap.rearrange("p t (c i) -> p c t i", i=run)
 
-        def along(pairs, g, width):
-            return pairs[:, g * PACK:(g + 1) * PACK, :].unsqueeze(1).to_broadcast([P, width // 2, PACK, 2])
+        def gain_along(g, width):
+            return gain_pairs[:, g * PACK:(g + 1) * PACK, :].unsqueeze(1).to_broadcast([P, width // 2, PACK, 2])
 
         win_codes = keep.tile([P, D], I32, name="win_codes", align_bytes=64)
         win_plane = keep.tile([P, D], U8, name="win_plane", align_bytes=64)
@@ -185,13 +187,16 @@ def tile_antisymmetricssprk2step_x2_kernel(tc, h, x, w, win_words, win_scales, b
         a_bf = {}
 
         def r_of(g, j):
-            return r_pairs[:, g * PACK + j, 0:1]
+            return r_f32[:, g, j:j + 1]
 
         def a_turn(g, gc, u):
             words = w_quad[gc, g][:].bitcast(F32)
             w_banks[g, gc, u] = new_bank()
             for t in range(PACK):
                 nc.tensor.transpose(w_banks[g, gc, u][:, t * P:(t + 1) * P], words[:, t, u::2], ident[:])
+
+        def turned_half(g, gc, u, e):
+            return w_banks[g, gc, u][:].bitcast(BF16).rearrange("p (c e) -> p c e", e=2)[:, :, e]
 
         def a_direct(g, gc, u):
             if (g, gc) not in rw:
@@ -208,9 +213,7 @@ def tile_antisymmetricssprk2step_x2_kernel(tc, h, x, w, win_words, win_scales, b
                 rwt[g, gc] = wide("rwt", GROUP)
             for e in range(2):
                 nc.scalar.activation(
-                    out=rwt[g, gc][:, 2 * u + e, :],
-                    in_=w_banks[g, gc, u][:].bitcast(BF16).rearrange("p (c e) -> p c e", e=2)[:, :, e],
-                    func=ACT.Copy, scale=r_of(g, 2 * u + e),
+                    out=rwt[g, gc][:, 2 * u + e, :], in_=turned_half(g, gc, u, e), func=ACT.Copy, scale=r_of(g, 2 * u + e)
                 )
 
         def a_subtract(g, gc):
@@ -220,6 +223,16 @@ def tile_antisymmetricssprk2step_x2_kernel(tc, h, x, w, win_words, win_scales, b
                 op=ALU.subtract,
             )
 
+        def a_finish(u):
+            if (0, 0) not in scaled:
+                scaled[0, 0] = staged("scaled", [P, PACK, GROUP], BF16)
+            for e in range(2):
+                j = 2 * u + e
+                nc.vector.scalar_tensor_tensor(
+                    out=scaled[0, 0][:, j, :], in0=turned_half(0, 0, u, e), scalar=minus_r[:, j:j + 1],
+                    in1=rw[0, 0][:, j, :], op0=ALU.mult, op1=ALU.add,
+                )
+
         def diff_subtract(g, gc, u):
             if (g, gc) not in diff:
                 diff[g, gc] = wide("diff", GROUP)
@@ -228,24 +241,6 @@ def tile_antisymmetricssprk2step_x2_kernel(tc, h, x, w, win_words, win_scales, b
                 in0=w_quad[g, gc][:, 2 * u:2 * u + 2, :].rearrange("p e (m t) -> p e t m", t=PACK),
                 in1=w_banks[g, gc, u][:].bitcast(BF16).rearrange("p (t m e) -> p e t m", t=PACK, e=2),
                 op=ALU.subtract,
-            )
-
-        def a_finish(u):
-            if (0, 0) not in scaled:
-                scaled[0, 0] = staged("scaled", [P, PACK, GROUP], BF16)
-            for e in range(2):
-                j = 2 * u + e
-                nc.vector.scalar_tensor_tensor(
-                    out=scaled[0, 0][:, j, :],
-                    in0=w_banks[0, 0, u][:].bitcast(BF16).rearrange("p (c e) -> p c e", e=2)[:, :, e],
-                    scalar=minus_r[:, j:j + 1], in1=rw[0, 0][:, j, :], op0=ALU.mult, op1=ALU.add,
-                )
-
-        def diff_gain(g, gc):
-            a_bf[g, gc] = staged("a_bf", [P, GROUP * PACK], BF16)
-            nc.vector.tensor_tensor(
-                out=interleaved(a_bf[g, gc][:], 2), in0=by_slot(diff[g, gc][:], 2), in1=along(r_pairs, g, GROUP),
-                op=ALU.mult,
             )
 
         def diff_scale(g, gc, u):
@@ -268,9 +263,10 @@ def tile_antisymmetricssprk2step_x2_kernel(tc, h, x, w, win_words, win_scales, b
                 out=scaled[0, 1][:, j, :], in_=diff_banks[j][:], func=ACT.Copy, scale=minus_r[:, j:j + 1]
             )
 
-        def a_interleave(g, gc):
+        def a_interleave(g, gc, on_vector):
             a_bf[g, gc] = staged("a_bf", [P, GROUP * PACK], BF16)
-            nc.vector.tensor_copy(out=interleaved(a_bf[g, gc][:], 4), in_=by_slot(scaled[g, gc][:], 4))
+            copy = nc.vector.tensor_copy if on_vector else nc.scalar.copy
+            copy(out=interleaved(a_bf[g, gc][:], 4), in_=by_slot(scaled[g, gc][:], 4))
 
         def a_quantize(g, gc):
             cols = slice(gc * GROUP, (gc + 1) * GROUP)
@@ -284,14 +280,14 @@ def tile_antisymmetricssprk2step_x2_kernel(tc, h, x, w, win_words, win_scales, b
             bank = new_bank()
             for u in range(2):
                 for i in range(2):
-                    slot = 2 * u + i
-                    nc.tensor.transpose(bank[:, slot * P:(slot + 1) * P], words_of(i, u), ident[:])
+                    place_in_bank = 2 * u + i
+                    nc.tensor.transpose(bank[:, place_in_bank * P:(place_in_bank + 1) * P], words_of(i, u), ident[:])
             return bank
 
         def h_turn(q, g):
             c, part = place(q)
             words = h_rows[c][:].bitcast(F32)
-            h_banks[q, g] = turn_words(lambda i, u: words[:, 2 * part + i, 256 * g + u:256 * (g + 1):2])
+            h_banks[q, g] = turn_words(lambda i, u: words[:, 2 * part + i, GROUP_WORDS * g + u:GROUP_WORDS * (g + 1):2])
 
         def h_gain(q, g):
             c, part = place(q)
@@ -323,11 +319,8 @@ def tile_antisymmetricssprk2step_x2_kernel(tc, h, x, w, win_words, win_scales, b
         x_banks = {}
         x_bf = {}
 
-        def keep_words(dst, bank):
-            nc.scalar.copy(out=dst, in_=bank[:].rearrange("p (u b) -> p b u", u=2))
-
         def as_values(words):
-            return words[:].rearrange("p b u -> p (b u)").bitcast(BF16)
+            return words.rearrange("p b u -> p (b u)").bitcast(BF16)
 
         def x_turn(q):
             words = x_rows[q][:].bitcast(F32)
@@ -343,7 +336,7 @@ def tile_antisymmetricssprk2step_x2_kernel(tc, h, x, w, win_words, win_scales, b
             )
 
         def x_quantize(c):
-            quantize(x_codes[:, batch(c)], x_plane[:, batch(c)], as_values(x_bf[c]))
+            quantize(x_codes[:, batch(c)], x_plane[:, batch(c)], as_values(x_bf[c][:]))
 
         z_banks = {}
         tanh_z = {}
@@ -375,34 +368,47 @@ def tile_antisymmetricssprk2step_x2_kernel(tc, h, x, w, win_words, win_scales, b
 
         up_bf = {}
 
-        def mid_update(c, g):
+        def make_y(dst, c, g):
             nc.vector.scalar_tensor_tensor(
-                out=mid[c, g][:], in0=tanh_z[0, c, g][:], scalar=0.75, in1=mid[c, g][:], op0=ALU.mult, op1=ALU.add
+                out=dst[:], in0=tanh_z[0, c, g][:], scalar=0.75, in1=mid[c, g][:], op0=ALU.mult, op1=ALU.add
             )
 
-        def mid_gain(c, g):
+        def make_up(y, c, g):
             if c not in up_bf:
                 up_bf[c] = staged_pair("up_bf", [P, GROUPS, CHUNKS[c][1] * PACK])
             nc.vector.tensor_tensor(
-                out=interleaved(up_bf[c][:, g, :], 2), in0=by_slot(mid[c, g][:], 2),
-                in1=along(gain_pairs, g, CHUNKS[c][1]), op=ALU.mult,
+                out=interleaved(up_bf[c][:, g, :], 2), in0=by_slot(y[:], 2), in1=gain_along(g, CHUNKS[c][1]), op=ALU.mult
             )
+
+        def mid_update(c, g):
+            make_y(mid[c, g], c, g)
+
+        def mid_gain(c, g):
+            make_up(mid[c, g], c, g)
 
         def mid_quantize(c):
             quantize_state(1, c, up_bf[c])
 
+        out_banks = {}
+        out_rows = {}
+        out_words = {}
+        plane_banks = {}
+        out_bf = {}
+
+        def row_tile(q, g, i):
+            c, part = place(q)
+            if (c, g) not in out_rows:
+                out_rows[c, g] = work.tile([P, CHUNKS[c][1] // P, GROUP], F32, name="out_rows", bufs=2)
+            return out_rows[c, g][:, 2 * part + i, :]
+
+        def features_in_order(bank):
+            return bank[:].rearrange("p (t m) -> p m t", t=PACK)
+
         def last_update(c, g):
-            nc.vector.scalar_tensor_tensor(
-                out=tanh_z[0, c, g][:], in0=tanh_z[0, c, g][:], scalar=0.75, in1=mid[c, g][:], op0=ALU.mult, op1=ALU.add
-            )
+            make_y(tanh_z[0, c, g], c, g)
 
         def last_gain(c, g):
-            if c not in up_bf:
-                up_bf[c] = staged_pair("up_bf", [P, GROUPS, CHUNKS[c][1] * PACK])
-            nc.vector.tensor_tensor(
-                out=interleaved(up_bf[c][:, g, :], 2), in0=by_slot(tanh_z[0, c, g][:], 2),
-                in1=along(gain_pairs, g, CHUNKS[c][1]), op=ALU.mult,
-            )
+            make_up(tanh_z[0, c, g], c, g)
 
         def last_carry(c, g):
             nc.vector.scalar_tensor_tensor(
@@ -414,13 +420,12 @@ def tile_antisymmetricssprk2step_x2_kernel(tc, h, x, w, win_words, win_scales, b
 
         def last_round(c, g, on_vector):
             out_bf[c, g] = staged("out_bf", [P, CHUNKS[c][1], 2], F32)
-            dst = interleaved(as_values(out_bf[c, g]), 2)
+            dst = interleaved(as_values(out_bf[c, g][:]), 2)
+            src = by_slot(tanh_z[1, c, g][:], 2)
             if on_vector:
-                nc.vector.tensor_scalar(
-                    out=dst, in0=by_slot(tanh_z[1, c, g][:], 2), scalar1=0.25, scalar2=None, op0=ALU.mult
-                )
+                nc.vector.tensor_scalar(out=dst, in0=src, scalar1=0.25, scalar2=None, op0=ALU.mult)
             else:
-                nc.scalar.activation(out=dst, in_=by_slot(tanh_z[1, c, g][:], 2), func=ACT.Copy, scale=0.25)
+                nc.scalar.activation(out=dst, in_=src, func=ACT.Copy, scale=0.25)
 
         def last_turn(q, g, i):
             c, part = place(q)
@@ -430,46 +435,33 @@ def tile_antisymmetricssprk2step_x2_kernel(tc, h, x, w, win_words, win_scales, b
                 nc.tensor.transpose(out_banks[q, g, i][:, t * P:(t + 1) * P], tanh_z[1, c, g][:, t, rows], ident[:])
 
         def last_keep(q, g, i):
-            c, part = place(q)
-            if (c, g) not in out_rows:
-                out_rows[c, g] = work.tile([P, CHUNKS[c][1] // P, GROUP], F32, name="out_rows", bufs=2)
             nc.scalar.activation(
-                out=out_rows[c, g][:, 2 * part + i, :].rearrange("p (m t) -> p m t", t=PACK),
-                in_=out_banks[q, g, i][:].rearrange("p (t m) -> p m t", t=PACK),
+                out=row_tile(q, g, i).rearrange("p (m t) -> p m t", t=PACK), in_=features_in_order(out_banks[q, g, i]),
                 func=ACT.Copy, scale=0.25,
             )
 
         def last_store(q, g, i):
-            c, part = place(q)
             first = q * QUARTER + i * P
-            nc.sync.dma_start(out=out_0[first:first + P, g * GROUP:(g + 1) * GROUP], in_=out_rows[c, g][:, 2 * part + i, :])
-
-        out_banks = {}
-        out_rows = {}
-        out_words = {}
-        plane_banks = {}
-        out_bf = {}
+            nc.sync.dma_start(out=out_0[first:first + P, g * GROUP:(g + 1) * GROUP], in_=row_tile(q, g, i))
 
         def out_turn(q, g, i):
             c, part = place(q)
             out_banks[q, g, i] = new_bank()
             rows = slice((2 * part + i) * P, (2 * part + i + 1) * P)
             for t in range(PACK):
-                slot = out_banks[q, g, i][:, t * P:(t + 1) * P]
+                summed = out_banks[q, g, i][:, t * P:(t + 1) * P]
                 nc.tensor.matmul(
-                    out=slot, lhsT=mid[c, g][:, t, rows], rhs=ident[:], is_transpose=True, start=True, stop=False
+                    out=summed, lhsT=mid[c, g][:, t, rows], rhs=ident[:], is_transpose=True, start=True, stop=False
                 )
                 nc.tensor.matmul(
-                    out=slot, lhsT=tanh_z[1, c, g][:, t, rows], rhs=ident[:], is_transpose=True, start=False, stop=True
+                    out=summed, lhsT=tanh_z[1, c, g][:, t, rows], rhs=ident[:], is_transpose=True, start=False, stop=True
                 )
 
         def out_update(q, g, i):
             c, part = place(q)
-            if (c, g) not in out_rows:
-                out_rows[c, g] = work.tile([P, CHUNKS[c][1] // P, GROUP], F32, name="out_rows", bufs=2)
             nc.vector.scalar_tensor_tensor(
-                out=out_rows[c, g][:, 2 * part + i, :].rearrange("p (m t) -> p m t", t=PACK),
-                in0=out_banks[q, g, i][:].rearrange("p (t m) -> p m t", t=PACK),
+                out=row_tile(q, g, i).rearrange("p (m t) -> p m t", t=PACK),
+                in0=features_in_order(out_banks[q, g, i]),
                 scalar=0.25,
                 in1=h_rows[c][:, 2 * part + i, g * GROUP:(g + 1) * GROUP].rearrange("p (m t) -> p m t", t=PACK),
                 op0=ALU.mult, op1=ALU.add,
@@ -482,16 +474,13 @@ def tile_antisymmetricssprk2step_x2_kernel(tc, h, x, w, win_words, win_scales, b
                 in_=out_rows[c, g][:, 2 * part:2 * part + 2, :],
             )
 
-        def out_round(q, g, quarters, on_vector):
+        def out_round(q, g, quarters):
             c, part = place(q)
             words = work.tile([P, 2, quarters * QUARTER, 2], BF16, name="out_words")
             for k in range(quarters):
                 out_words[q + k, g] = words[:].rearrange("p u m e -> p u (m e)").bitcast(F32)[:, :, rows_of(k)]
             src = out_rows[c, g][:, 2 * part:2 * (part + quarters), :].rearrange("p i (m u e) -> p u (i m) e", u=2, e=2)
-            if on_vector:
-                nc.vector.tensor_copy(out=words[:], in_=src)
-            else:
-                nc.scalar.copy(out=words[:], in_=src)
+            nc.scalar.copy(out=words[:], in_=src)
 
         def plane_turn(q, g):
             plane_banks[q, g] = turn_words(lambda i, u: out_words[q, g][:, u, i * P:(i + 1) * P])
@@ -500,233 +489,73 @@ def tile_antisymmetricssprk2step_x2_kernel(tc, h, x, w, win_words, win_scales, b
             c, part = place(q)
             if (c, g) not in out_bf:
                 out_bf[c, g] = staged("out_bf", [P, CHUNKS[c][1], 2], F32)
-            keep_words(out_bf[c, g][:, rows_of(part), :], plane_banks[q, g])
+            nc.scalar.copy(
+                out=out_bf[c, g][:, rows_of(part), :], in_=plane_banks[q, g][:].rearrange("p (u b) -> p b u", u=2)
+            )
 
         def out_planes(q, g, quarters):
             c, part = place(q)
             cols = slice(q * QUARTER, (q + quarters) * QUARTER)
             codes = work.tile([P, quarters * QUARTER], U32, name="out_codes", align_bytes=64)
             values = out_bf[c, g][:, part * QUARTER:(part + quarters) * QUARTER, :]
-            quantize(codes[:], out_plane[:, g, cols], values.rearrange("p b u -> p (b u)").bitcast(BF16))
+            quantize(codes[:], out_plane[:, g, cols], as_values(values))
             nc.sync.dma_start(out=out_1[g].rearrange("p m t -> p (m t)").bitcast(I32)[:, cols], in_=codes[:].bitcast(I32))
 
-        def out_scales(g):
+        def out_scales(g, engine):
             for quad in range(4):
-                nc.sync.dma_start(
+                engine.dma_start(
                     out=out_2[g, 4 * quad:4 * quad + 4, :].bitcast(I32),
                     in_=out_plane[32 * quad:32 * quad + 4, g, :].bitcast(I32),
                 )
 
+        order = [
+            (a_turn, 0, 0, 0), (a_direct, 0, 0, 0), (a_finish, 0), (a_turn, 0, 0, 1), (h_turn, 0, 1),
+            (a_direct, 0, 0, 1), (a_finish, 1), (h_keep, 0, 1), (a_interleave, 0, 0, ON_SCALAR), (h_turn, 0, 0),
+            (h_gain, 0, 0), (a_turn, 1, 0, 0), (h_gain, 0, 1), (a_turn, 1, 0, 1), (x_turn, 0), (h_turn, 1, 0),
+            (diff_subtract, 1, 0, 0), (h_keep, 0, 0), (diff_scale, 1, 0, 0), (h_turn, 1, 1),
+            (diff_subtract, 1, 0, 1), (diff_scale, 1, 0, 1), (diff_turn, 0), (x_keep, 0), (diff_turn, 2),
+            (diff_turned, 0), (x_turn, 1), (win_move_codes,), (x_keep, 1), (a_quantize, 0, 0), (win_move_scales,),
+            (h_gain, 1, 1), (h_gain, 1, 0), (diff_turn, 1), (diff_turned, 2), (h_turn, 2, 0), (diff_turn, 3),
+            (h_turn, 3, 0), (a_interleave, 1, 0, ON_VECTOR), (a_turn, 1, 1, 0), (h_quantize, 0), (diff_turned, 1),
+            (a_quantize, 1, 0), (x_quantize, 0), (diff_turned, 3), (h_gain, 3, 0), (a_interleave, 0, 1, ON_VECTOR),
+            (h_turn, 2, 1), (a_direct, 1, 1, 0), (h_gain, 2, 0), (h_gain, 2, 1), (a_turned, 1, 1, 0), (h_turn, 3, 1),
+            (a_turn, 1, 1, 1), (h_gain, 3, 1), (a_direct, 1, 1, 1), (a_turned, 1, 1, 1), (h_quantize, 1),
+            (h_keep, 1, 0), (z_matmul, 0, 0, 0, 0), (h_quantize, 2), (z_tanh, 0, 0, 0, 0), (z_matmul, 0, 0, 0, 1),
+            (z_tanh, 0, 0, 0, 1), (a_subtract, 1, 1), (a_quantize, 0, 1), (a_quantize, 1, 1), (x_turn, 2),
+            (x_keep, 2), (z_matmul, 0, 0, 1, 0), (mid_update, 0, 0), (h_keep, 1, 1), (z_matmul, 0, 0, 1, 1),
+            (x_quantize, 1), (mid_gain, 0, 0), (z_tanh, 0, 0, 1, 0), (z_tanh, 0, 0, 1, 1), (mid_update, 0, 1),
+            (x_turn, 3), (x_keep, 3), (x_quantize, 2), (z_matmul, 0, 1, 1, 0), (mid_gain, 0, 1),
+            (z_matmul, 0, 1, 0, 0), (z_tanh, 0, 1, 1, 0), (z_matmul, 0, 1, 1, 1), (h_keep, 2, 0),
+            (z_tanh, 0, 1, 1, 1), (z_matmul, 0, 1, 0, 1), (z_tanh, 0, 1, 0, 0), (z_tanh, 0, 1, 0, 1),
+            (z_matmul, 0, 2, 1, 0), (z_matmul, 0, 2, 0, 1), (h_halve, 1), (mid_quantize, 0), (mid_update, 1, 0),
+            (h_keep, 2, 1), (z_matmul, 0, 2, 0, 0), (z_tanh, 0, 2, 0, 0), (z_tanh, 0, 2, 1, 0), (z_tanh, 0, 2, 0, 1),
+            (h_halve, 0), (z_matmul, 0, 2, 1, 1), (z_matmul, 1, 0, 0, 0), (z_tanh, 1, 0, 0, 0), (h_keep, 3, 1),
+            (z_matmul, 1, 0, 0, 1), (z_matmul, 1, 0, 1, 0), (last_update, 1, 1), (z_tanh, 1, 0, 0, 1),
+            (out_turn, 0, 0, 0), (z_tanh, 1, 0, 1, 0), (mid_gain, 1, 0), (h_keep, 3, 0), (last_gain, 1, 1),
+            (out_turn, 1, 0, 0), (last_carry, 1, 1), (z_tanh, 0, 2, 1, 1), (out_turn, 1, 0, 1), (out_turn, 0, 0, 1),
+            (mid_quantize, 1), (z_matmul, 1, 1, 1, 0), (z_tanh, 1, 1, 1, 0), (out_update, 0, 0, 0),
+            (out_update, 1, 0, 1), (out_update, 1, 0, 0), (out_update, 0, 0, 1), (out_store, 0, 0),
+            (z_matmul, 1, 1, 1, 1), (z_tanh, 1, 1, 1, 1), (z_matmul, 1, 0, 1, 1), (last_update, 2, 0),
+            (out_round, 0, 0, 2), (z_tanh, 1, 0, 1, 1), (z_matmul, 1, 1, 0, 0), (last_sum, 1, 1),
+            (last_turn, 2, 1, 1), (last_turn, 2, 1, 0), (out_store, 1, 0), (last_keep, 2, 1, 0), (last_update, 2, 1),
+            (plane_turn, 0, 0), (out_turn, 1, 1, 0), (out_turn, 0, 1, 0), (out_turn, 1, 1, 1), (last_gain, 2, 0),
+            (last_keep, 2, 1, 1), (last_gain, 2, 1), (plane_turn, 1, 0), (last_store, 2, 1, 1),
+            (out_update, 0, 1, 0), (out_update, 1, 1, 1), (out_update, 1, 1, 0), (plane_keep, 0, 0),
+            (last_round, 1, 1, ON_SCALAR), (last_store, 2, 1, 0), (plane_keep, 1, 0), (out_turn, 0, 1, 1),
+            (z_matmul, 1, 1, 0, 1), (z_tanh, 1, 1, 0, 0), (z_tanh, 1, 1, 0, 1), (mid_quantize, 2),
+            (out_update, 0, 1, 1), (out_store, 0, 1), (out_planes, 2, 1, 1), (out_round, 0, 1, 2),
+            (out_turn, 2, 0, 1), (out_turn, 2, 0, 0), (last_carry, 2, 1), (out_store, 1, 1), (out_planes, 0, 0, 2),
+            (last_carry, 2, 0), (z_matmul, 1, 2, 1, 0), (z_tanh, 1, 2, 1, 0), (z_matmul, 1, 2, 1, 1),
+            (plane_turn, 0, 1), (out_update, 2, 0, 0), (out_update, 2, 0, 1), (out_store, 2, 0),
+            (z_tanh, 1, 2, 1, 1), (plane_turn, 1, 1), (z_matmul, 1, 2, 0, 0), (plane_keep, 0, 1), (last_sum, 2, 1),
+            (plane_keep, 1, 1), (z_tanh, 1, 2, 0, 0), (out_planes, 0, 1, 2), (z_matmul, 1, 2, 0, 1),
+            (last_turn, 3, 1, 0), (z_tanh, 1, 2, 0, 1), (last_turn, 3, 1, 1), (last_keep, 3, 1, 0),
+            (last_store, 3, 1, 0), (last_round, 2, 1, ON_VECTOR), (out_round, 2, 0, 1), (last_keep, 3, 1, 1),
+            (last_sum, 2, 0), (last_turn, 3, 0, 0), (out_planes, 3, 1, 1), (out_scales, 1, nc.sync),
+            (last_store, 3, 1, 1), (plane_turn, 2, 0), (last_turn, 3, 0, 1), (last_keep, 3, 0, 0),
+            (last_round, 2, 0, ON_VECTOR), (last_keep, 3, 0, 1), (last_store, 3, 0, 0), (last_store, 3, 0, 1),
+            (out_planes, 3, 0, 1), (plane_keep, 2, 0), (out_planes, 2, 0, 1), (out_scales, 0, nc.scalar),
+        ]
         ctx.enter_context(tc.manual_schedule())
-        a_direct(0, 0, 0)
-        a_turn(0, 0, 0)
-        a_finish(0)
-        a_turn(0, 0, 1)
-        a_direct(0, 0, 1)
-        a_finish(1)
-        h_turn(0, 0)
-        h_gain(0, 0)
-        h_keep(0, 0)
-        h_turn(0, 1)
-        a_turn(1, 0, 0)
-        a_turn(1, 0, 1)
-        h_keep(0, 1)
-        x_turn(0)
-        a_interleave(0, 0)
-        diff_subtract(1, 0, 0)
-        diff_subtract(1, 0, 1)
-        h_turn(1, 0)
-        win_move_scales()
-        diff_scale(1, 0, 0)
-        diff_scale(1, 0, 1)
-        h_gain(0, 1)
-        h_turn(1, 1)
-        h_gain(1, 0)
-        diff_turn(2)
-        a_direct(1, 1, 0)
-        x_keep(0)
-        h_gain(1, 1)
-        x_turn(1)
-        diff_turn(0)
-        diff_turn(3)
-        x_keep(1)
-        diff_turned(0)
-        diff_turned(3)
-        diff_turned(2)
-        a_interleave(1, 0)
-        a_turn(1, 1, 0)
-        diff_turn(1)
-        diff_turned(1)
-        a_turned(1, 1, 0)
-        a_turn(1, 1, 1)
-        h_quantize(0)
-        x_quantize(0)
-        h_turn(2, 0)
-        a_quantize(1, 0)
-        h_turn(2, 1)
-        a_turned(1, 1, 1)
-        win_move_codes()
-        a_direct(1, 1, 1)
-        a_quantize(0, 0)
-        h_keep(1, 0)
-        z_matmul(0, 0, 0, 0)
-        h_gain(2, 0)
-        a_interleave(0, 1)
-        h_gain(2, 1)
-        a_quantize(0, 1)
-        h_quantize(1)
-        z_tanh(0, 0, 0, 0)
-        x_turn(2)
-        a_subtract(1, 1)
-        h_turn(3, 0)
-        h_gain(3, 0)
-        h_turn(3, 1)
-        h_gain(3, 1)
-        h_keep(1, 1)
-        a_quantize(1, 1)
-        h_quantize(2)
-        z_matmul(0, 0, 0, 1)
-        z_tanh(0, 0, 0, 1)
-        mid_update(0, 0)
-        h_keep(2, 1)
-        x_keep(2)
-        x_quantize(1)
-        z_matmul(0, 0, 1, 0)
-        z_tanh(0, 0, 1, 0)
-        z_matmul(0, 0, 1, 1)
-        z_tanh(0, 0, 1, 1)
-        mid_gain(0, 0)
-        mid_update(0, 1)
-        x_turn(3)
-        h_keep(2, 0)
-        x_keep(3)
-        x_quantize(2)
-        z_matmul(0, 1, 1, 1)
-        z_matmul(0, 1, 1, 0)
-        z_tanh(0, 1, 1, 0)
-        z_matmul(0, 1, 0, 1)
-        mid_gain(0, 1)
-        z_matmul(0, 1, 0, 0)
-        mid_quantize(0)
-        z_tanh(0, 1, 1, 1)
-        last_update(1, 1)
-        z_tanh(0, 1, 0, 0)
-        z_matmul(0, 2, 0, 0)
-        h_keep(3, 1)
-        z_tanh(0, 2, 0, 0)
-        z_tanh(0, 1, 0, 1)
-        mid_update(1, 0)
-        h_halve(1)
-        z_matmul(0, 2, 1, 0)
-        z_tanh(0, 2, 1, 0)
-        z_matmul(0, 2, 0, 1)
-        z_matmul(0, 2, 1, 1)
-        mid_gain(1, 0)
-        last_gain(1, 1)
-        z_matmul(1, 0, 1, 1)
-        last_carry(1, 1)
-        z_tanh(0, 2, 0, 1)
-        h_keep(3, 0)
-        z_matmul(1, 0, 1, 0)
-        z_tanh(1, 0, 1, 0)
-        z_matmul(1, 0, 0, 0)
-        z_tanh(1, 0, 1, 1)
-        out_turn(0, 1, 1)
-        out_turn(1, 1, 1)
-        z_tanh(1, 0, 0, 0)
-        out_turn(0, 1, 0)
-        h_halve(0)
-        mid_quantize(1)
-        z_tanh(0, 2, 1, 1)
-        out_update(0, 1, 0)
-        out_update(0, 1, 1)
-        out_turn(1, 1, 0)
-        out_update(1, 1, 0)
-        z_matmul(1, 1, 0, 0)
-        z_tanh(1, 1, 0, 0)
-        out_update(1, 1, 1)
-        out_store(0, 1)
-        last_update(2, 1)
-        z_matmul(1, 1, 0, 1)
-        last_update(2, 0)
-        z_matmul(1, 1, 1, 0)
-        z_tanh(1, 1, 0, 1)
-        out_turn(2, 0, 0)
-        out_update(2, 0, 0)
-        out_turn(2, 0, 1)
-        out_update(2, 0, 1)
-        z_matmul(1, 1, 1, 1)
-        out_store(1, 1)
-        out_round(0, 1, 2, False)
-        last_gain(2, 0)
-        out_store(2, 0)
-        z_tanh(1, 1, 1, 0)
-        z_tanh(1, 1, 1, 1)
-        out_round(2, 0, 1, False)
-        z_matmul(1, 0, 0, 1)
-        z_tanh(1, 0, 0, 1)
-        plane_turn(1, 1)
-        last_sum(1, 1)
-        plane_turn(0, 1)
-        plane_turn(2, 0)
-        last_turn(2, 1, 0)
-        plane_keep(2, 0)
-        last_keep(2, 1, 0)
-        plane_keep(0, 1)
-        last_store(2, 1, 0)
-        last_gain(2, 1)
-        last_carry(2, 1)
-        out_turn(0, 0, 0)
-        out_turn(1, 0, 0)
-        out_planes(2, 0, 1)
-        last_turn(2, 1, 1)
-        mid_quantize(2)
-        out_update(0, 0, 0)
-        out_update(1, 0, 0)
-        out_turn(0, 0, 1)
-        out_turn(1, 0, 1)
-        out_update(1, 0, 1)
-        out_store(1, 0)
-        last_round(1, 1, False)
-        plane_keep(1, 1)
-        last_keep(2, 1, 1)
-        z_matmul(1, 2, 1, 0)
-        out_planes(2, 1, 1)
-        z_tanh(1, 2, 1, 0)
-        last_store(2, 1, 1)
-        z_matmul(1, 2, 1, 1)
-        z_tanh(1, 2, 1, 1)
-        z_matmul(1, 2, 0, 0)
-        out_update(0, 0, 1)
-        out_store(0, 0)
-        z_matmul(1, 2, 0, 1)
-        last_carry(2, 0)
-        out_round(0, 0, 2, False)
-        z_tanh(1, 2, 0, 0)
-        z_tanh(1, 2, 0, 1)
-        last_sum(2, 1)
-        last_turn(3, 1, 0)
-        last_keep(3, 1, 0)
-        last_turn(3, 1, 1)
-        out_planes(0, 1, 2)
-        last_round(2, 1, True)
-        out_planes(3, 1, 1)
-        last_sum(2, 0)
-        last_keep(3, 1, 1)
-        out_scales(1)
-        last_store(3, 1, 1)
-        plane_turn(1, 0)
-        plane_turn(0, 0)
-        plane_keep(0, 0)
-        plane_keep(1, 0)
-        last_round(2, 0, True)
-        last_store(3, 1, 0)
-        last_turn(3, 0, 0)
-        out_planes(3, 0, 1)
-        last_keep(3, 0, 0)
-        last_store(3, 0, 0)
-        last_turn(3, 0, 1)
-        last_keep(3, 0, 1)
-        last_store(3, 0, 1)
-        out_planes(0, 0, 2)
-        out_scales(0)
+        for step, *args in order:
+            step(*args)

from contextlib import ExitStack

import concourse.mybir as mybir
from concourse.masks import make_identity

B, D, X = 1024, 1024, 512
FLOPS = 2 * B * D * (X + 2 * D)

F32 = mybir.dt.float32
BF16 = mybir.dt.bfloat16
I32 = mybir.dt.int32
U32 = mybir.dt.uint32
U8 = mybir.dt.uint8
FP8X4 = mybir.dt.float8_e4m3fn_x4
ACT = mybir.ActivationFunctionType
ALU = mybir.AluOpType

P = 128
PACK = 4
GROUP = P * PACK
GROUPS = D // GROUP
GROUP_WORDS = GROUP // 2
BANK = 512
QUARTER = 256
CHUNKS = [(0, 512), (512, 256), (768, 256)]
STAGED_BUFS = 5
WIDE_BUFS = 5
ON_VECTOR, ON_SCALAR = True, False


def tile_antisymmetricssprk2step_x2_kernel(tc, h, x, w, win_words, win_scales, b, p, r, out_0, out_1, out_2):
    nc = tc.nc
    with ExitStack() as ctx:
        keep = ctx.enter_context(tc.tile_pool(name="keep", bufs=1))
        work = ctx.enter_context(tc.tile_pool(name="work", bufs=2))
        psum = ctx.enter_context(tc.psum_pool(name="psum", bufs=8))

        def new_bank():
            return psum.tile([P, BANK], F32, name="bank")

        def staged(name, shape, dtype):
            return work.tile(shape, dtype, name=name, tag="staged", bufs=STAGED_BUFS, align_bytes=64)

        def staged_pair(name, shape):
            return work.tile(shape, BF16, name=name, tag="staged_pair", bufs=2, align_bytes=64)

        def wide(name, width):
            return work.tile([P, PACK, width], F32, name=name, tag="wide", bufs=WIDE_BUFS)

        def quantize(codes, scales, values):
            nc.vector.quantize_mx(out=codes.bitcast(FP8X4), scales=scales, in_=values)

        def place(q):
            for c, (first, width) in enumerate(CHUNKS):
                if first <= q * QUARTER < first + width:
                    return c, (q * QUARTER - first) // QUARTER

        def batch(c):
            return slice(CHUNKS[c][0], CHUNKS[c][0] + CHUNKS[c][1])

        def rows_of(part):
            return slice(part * QUARTER, (part + 1) * QUARTER)

        ident = keep.tile([P, P], F32, name="ident")
        make_identity(nc, ident[:])

        w_quad = {}
        h_rows = {}
        x_rows = {}

        def load_w(g, gc, pieces):
            w_quad[g, gc] = keep.tile([P, PACK, GROUP], BF16, name="w_%d_%d" % (g, gc))
            rows = w[g * GROUP:(g + 1) * GROUP, gc * GROUP:(gc + 1) * GROUP].rearrange("(p j) n -> p j n", j=PACK)
            step = PACK // pieces
            for j in range(0, PACK, step):
                nc.sync.dma_start(out=w_quad[g, gc][:, j:j + step, :], in_=rows[:, j:j + step, :])

        def load_h(q):
            c, part = place(q)
            if c not in h_rows:
                h_rows[c] = keep.tile([P, CHUNKS[c][1] // P, D], BF16, name="h_%d" % c)
            nc.sync.dma_start(
                out=h_rows[c][:, 2 * part:2 * part + 2, :], in_=h[rows_of(q), :].rearrange("(i p) d -> p i d", p=P)
            )

        def load_x(q):
            x_rows[q] = keep.tile([P, 2, X], BF16, name="x_%d" % q)
            nc.sync.dma_start(out=x_rows[q][:], in_=x[rows_of(q), :].rearrange("(p i) k -> p i k", p=P))

        def load_vector(engine, vec, name):
            loaded = keep.tile([P, GROUPS, PACK], BF16, name=name)
            engine.dma_start(out=loaded[:], in_=vec.rearrange("(g p t) -> p g t", g=GROUPS, t=PACK))
            return loaded

        win_raw = keep.tile([P, D], I32, name="win_raw")
        win_raw_scales = keep.tile([P, D], U8, name="win_raw_scales")
        nc.vector.memset(win_raw_scales[:].bitcast(I32), 0)

        def load_win():
            nc.sync.dma_start(out=win_raw[:], in_=win_words[0].rearrange("p n t -> p (n t)").bitcast(I32))

        def load_win_scales():
            for quad in range(4):
                nc.sync.dma_start(
                    out=win_raw_scales[32 * quad:32 * quad + 4, :].bitcast(I32),
                    in_=win_scales[0, 4 * quad:4 * quad + 4, :].bitcast(I32),
                )

        r_bf = load_vector(nc.scalar, r, "r_bf")
        p_bf = load_vector(nc.scalar, p, "p_bf")
        load_w(0, 0, 2)
        load_h(0)
        load_w(1, 0, 1)
        load_w(0, 1, 1)
        load_x(0)
        load_win()
        load_win_scales()
        load_h(1)
        load_w(1, 1, 1)
        load_x(1)
        b_bf = load_vector(nc.sync, b, "b_bf")
        load_h(2)
        load_x(2)
        load_h(3)
        load_x(3)

        r_f32 = keep.tile([P, GROUPS, PACK], F32, name="r_f32")
        nc.vector.tensor_copy(out=r_f32[:], in_=r_bf[:])
        minus_r = keep.tile([P, PACK], F32, name="minus_r")
        nc.vector.tensor_scalar(out=minus_r[:], in0=r_bf[:, 0, :], scalar1=-1.0, scalar2=None, op0=ALU.mult)
        gain_pairs = keep.tile([P, GROUPS * PACK, 2], F32, name="gain_pairs")
        nc.vector.tensor_scalar(
            out=gain_pairs[:],
            in0=p_bf[:].rearrange("p g t -> p (g t)").unsqueeze(2).to_broadcast([P, GROUPS * PACK, 2]),
            scalar1=2.0 / 3.0, scalar2=None, op0=ALU.mult,
        )

        def interleaved(tile_ap, run):
            return tile_ap.rearrange("p (c i t) -> p c t i", i=run, t=PACK)

        def by_slot(tile_ap, run):
            return tile_ap.rearrange("p t (c i) -> p c t i", i=run)

        def gain_along(g, width):
            return gain_pairs[:, g * PACK:(g + 1) * PACK, :].unsqueeze(1).to_broadcast([P, width // 2, PACK, 2])

        win_codes = keep.tile([P, D], I32, name="win_codes", align_bytes=64)
        win_plane = keep.tile([P, D], U8, name="win_plane", align_bytes=64)

        def win_move_codes():
            nc.vector.tensor_copy(
                out=win_codes[:].rearrange("p (g t c i) -> p g c t i", g=GROUPS, t=PACK, i=4),
                in_=win_raw[:].rearrange("p (g c i t) -> p g c t i", g=GROUPS, t=PACK, i=4),
            )

        def win_move_scales():
            nc.vector.tensor_copy(
                out=win_plane[:].rearrange("p (g t m) -> p g t m", g=GROUPS, t=PACK),
                in_=win_raw_scales[:].rearrange("p (g m t) -> p g t m", g=GROUPS, t=PACK),
            )

        a_codes = keep.tile([P, GROUPS, D], U32, name="a_codes", align_bytes=64)
        a_plane = keep.tile([P, GROUPS, D], U8, name="a_plane", align_bytes=64)
        x_codes = keep.tile([P, B], U32, name="x_codes", align_bytes=64)
        x_plane = keep.tile([P, B], U8, name="x_plane", align_bytes=64)
        out_plane = keep.tile([P, GROUPS, B], U8, name="out_plane", align_bytes=64)
        s_codes = {}
        s_plane = {}
        for stage in range(2):
            for c, (first, width) in enumerate(CHUNKS):
                s_codes[stage, c] = keep.tile([P, GROUPS, width], U32, name="s_codes_%d_%d" % (stage, c), align_bytes=64)
                s_plane[stage, c] = keep.tile([P, GROUPS, width], U8, name="s_plane_%d_%d" % (stage, c), align_bytes=64)

        def quantize_state(stage, c, values):
            quantize(
                s_codes[stage, c][:].rearrange("p g b -> p (g b)"),
                s_plane[stage, c][:].rearrange("p g b -> p (g b)"),
                values[:].rearrange("p g n -> p (g n)"),
            )

        w_banks = {}
        rw = {}
        rwt = {}
        diff = {}
        scaled = {}
        diff_banks = {}
        a_bf = {}

        def r_of(g, j):
            return r_f32[:, g, j:j + 1]

        def a_turn(g, gc, u):
            words = w_quad[gc, g][:].bitcast(F32)
            w_banks[g, gc, u] = new_bank()
            for t in range(PACK):
                nc.tensor.transpose(w_banks[g, gc, u][:, t * P:(t + 1) * P], words[:, t, u::2], ident[:])

        def turned_half(g, gc, u, e):
            return w_banks[g, gc, u][:].bitcast(BF16).rearrange("p (c e) -> p c e", e=2)[:, :, e]

        def a_direct(g, gc, u):
            if (g, gc) not in rw:
                rw[g, gc] = wide("rw", GROUP)
            for j in (2 * u, 2 * u + 1):
                nc.scalar.activation(
                    out=rw[g, gc][:, j, :].rearrange("p (t m) -> p t m", t=PACK),
                    in_=w_quad[g, gc][:, j, :].rearrange("p (m t) -> p t m", t=PACK),
                    func=ACT.Copy, scale=r_of(g, j),
                )

        def a_turned(g, gc, u):
            if (g, gc) not in rwt:
                rwt[g, gc] = wide("rwt", GROUP)
            for e in range(2):
                nc.scalar.activation(
                    out=rwt[g, gc][:, 2 * u + e, :], in_=turned_half(g, gc, u, e), func=ACT.Copy, scale=r_of(g, 2 * u + e)
                )

        def a_subtract(g, gc):
            a_bf[g, gc] = staged("a_bf", [P, GROUP * PACK], BF16)
            nc.vector.tensor_tensor(
                out=interleaved(a_bf[g, gc][:], 2), in0=by_slot(rw[g, gc][:], 2), in1=by_slot(rwt[g, gc][:], 2),
                op=ALU.subtract,
            )

        def a_finish(u):
            if (0, 0) not in scaled:
                scaled[0, 0] = staged("scaled", [P, PACK, GROUP], BF16)
            for e in range(2):
                j = 2 * u + e
                nc.vector.scalar_tensor_tensor(
                    out=scaled[0, 0][:, j, :], in0=turned_half(0, 0, u, e), scalar=minus_r[:, j:j + 1],
                    in1=rw[0, 0][:, j, :], op0=ALU.mult, op1=ALU.add,
                )

        def diff_subtract(g, gc, u):
            if (g, gc) not in diff:
                diff[g, gc] = wide("diff", GROUP)
            nc.vector.tensor_tensor(
                out=diff[g, gc][:, 2 * u:2 * u + 2, :].rearrange("p e (t m) -> p e t m", t=PACK),
                in0=w_quad[g, gc][:, 2 * u:2 * u + 2, :].rearrange("p e (m t) -> p e t m", t=PACK),
                in1=w_banks[g, gc, u][:].bitcast(BF16).rearrange("p (t m e) -> p e t m", t=PACK, e=2),
                op=ALU.subtract,
            )

        def diff_scale(g, gc, u):
            if (g, gc) not in scaled:
                scaled[g, gc] = staged("scaled", [P, PACK, GROUP], BF16)
            for j in (2 * u, 2 * u + 1):
                nc.scalar.activation(
                    out=scaled[g, gc][:, j, :], in_=diff[g, gc][:, j, :], func=ACT.Copy, scale=r_of(g, j)
                )

        def diff_turn(j):
            diff_banks[j] = new_bank()
            for t in range(PACK):
                nc.tensor.transpose(diff_banks[j][:, t * P:(t + 1) * P], diff[1, 0][:, t, j * P:(j + 1) * P], ident[:])

        def diff_turned(j):
            if (0, 1) not in scaled:
                scaled[0, 1] = staged("scaled", [P, PACK, GROUP], BF16)
            nc.scalar.activation(
                out=scaled[0, 1][:, j, :], in_=diff_banks[j][:], func=ACT.Copy, scale=minus_r[:, j:j + 1]
            )

        def a_interleave(g, gc, on_vector):
            a_bf[g, gc] = staged("a_bf", [P, GROUP * PACK], BF16)
            copy = nc.vector.tensor_copy if on_vector else nc.scalar.copy
            copy(out=interleaved(a_bf[g, gc][:], 4), in_=by_slot(scaled[g, gc][:], 4))

        def a_quantize(g, gc):
            cols = slice(gc * GROUP, (gc + 1) * GROUP)
            quantize(a_codes[:, g, cols], a_plane[:, g, cols], a_bf[g, gc][:])

        mid = {}
        hp_bf = {}
        h_banks = {}

        def turn_words(words_of):
            bank = new_bank()
            for u in range(2):
                for i in range(2):
                    place_in_bank = 2 * u + i
                    nc.tensor.transpose(bank[:, place_in_bank * P:(place_in_bank + 1) * P], words_of(i, u), ident[:])
            return bank

        def h_turn(q, g):
            c, part = place(q)
            words = h_rows[c][:].bitcast(F32)
            h_banks[q, g] = turn_words(lambda i, u: words[:, 2 * part + i, GROUP_WORDS * g + u:GROUP_WORDS * (g + 1):2])

        def h_gain(q, g):
            c, part = place(q)
            if c not in hp_bf:
                hp_bf[c] = staged_pair("hp_bf", [P, GROUPS, CHUNKS[c][1] * PACK])
            nc.vector.tensor_tensor(
                out=hp_bf[c][:, g, :].rearrange("p (b u e) -> p b u e", u=2, e=2)[:, rows_of(part)],
                in0=h_banks[q, g][:].bitcast(BF16).rearrange("p (u b e) -> p b u e", u=2, e=2),
                in1=p_bf[:, g, :].rearrange("p (u e) -> p u e", e=2).unsqueeze(1).to_broadcast([P, QUARTER, 2, 2]),
                op=ALU.mult,
            )

        def h_keep(q, g):
            c, part = place(q)
            if (c, g) not in mid:
                mid[c, g] = keep.tile([P, PACK, CHUNKS[c][1]], F32, name="mid_%d_%d" % (c, g))
            nc.scalar.activation(
                out=mid[c, g][:, :, rows_of(part)].rearrange("p (u e) b -> p u e b", e=2),
                in_=h_banks[q, g][:].bitcast(BF16).rearrange("p (u b e) -> p u e b", u=2, e=2),
                func=ACT.Copy, scale=1.125,
            )

        def h_halve(c):
            nc.vector.tensor_scalar(out=h_rows[c][:], in0=h_rows[c][:], scalar1=0.5, scalar2=None, op0=ALU.mult)

        def h_quantize(c):
            quantize_state(0, c, hp_bf[c])

        x_banks = {}
        x_bf = {}

        def as_values(words):
            return words.rearrange("p b u -> p (b u)").bitcast(BF16)

        def x_turn(q):
            words = x_rows[q][:].bitcast(F32)
            x_banks[q] = turn_words(lambda i, u: words[:, i, u::2])

        def x_keep(q):
            c, part = place(q)
            if c not in x_bf:
                x_bf[c] = staged("x_bf", [P, CHUNKS[c][1], 2], F32)
            nc.scalar.copy(
                out=x_bf[c][:, rows_of(part), :].rearrange("p (b i) u -> p b i u", i=2),
                in_=x_banks[q][:].rearrange("p (u i b) -> p b i u", u=2, i=2),
            )

        def x_quantize(c):
            quantize(x_codes[:, batch(c)], x_plane[:, batch(c)], as_values(x_bf[c][:]))

        z_banks = {}
        tanh_z = {}

        def z_matmul(stage, c, g, u):
            for t in (2 * u, 2 * u + 1):
                ch = slice(g * GROUP + t * P, g * GROUP + (t + 1) * P)
                bank = new_bank()
                z = bank[:, :CHUNKS[c][1]]
                z_banks[stage, c, g, t] = z
                nc.tensor.matmul_mx(
                    out=z, lhsT=win_codes[:, ch].bitcast(FP8X4), lhsT_scale=win_plane[:, ch],
                    rhs=x_codes[:, batch(c)].bitcast(FP8X4), rhs_scale=x_plane[:, batch(c)], start=True, stop=False,
                )
                for kg in range(GROUPS):
                    nc.tensor.matmul_mx(
                        out=z, lhsT=a_codes[:, kg, ch].bitcast(FP8X4), lhsT_scale=a_plane[:, kg, ch],
                        rhs=s_codes[stage, c][:, kg, :].bitcast(FP8X4), rhs_scale=s_plane[stage, c][:, kg, :],
                        start=False, stop=(kg == GROUPS - 1),
                    )

        def z_tanh(stage, c, g, u):
            if (stage, c, g) not in tanh_z:
                tanh_z[stage, c, g] = wide("tanh_z", CHUNKS[c][1])
            for t in (2 * u, 2 * u + 1):
                nc.scalar.activation(
                    out=tanh_z[stage, c, g][:, t, :], in_=z_banks[stage, c, g, t], func=ACT.Tanh, bias=b_bf[:, g, t:t + 1]
                )

        up_bf = {}

        def make_y(dst, c, g):
            nc.vector.scalar_tensor_tensor(
                out=dst[:], in0=tanh_z[0, c, g][:], scalar=0.75, in1=mid[c, g][:], op0=ALU.mult, op1=ALU.add
            )

        def make_up(y, c, g):
            if c not in up_bf:
                up_bf[c] = staged_pair("up_bf", [P, GROUPS, CHUNKS[c][1] * PACK])
            nc.vector.tensor_tensor(
                out=interleaved(up_bf[c][:, g, :], 2), in0=by_slot(y[:], 2), in1=gain_along(g, CHUNKS[c][1]), op=ALU.mult
            )

        def mid_update(c, g):
            make_y(mid[c, g], c, g)

        def mid_gain(c, g):
            make_up(mid[c, g], c, g)

        def mid_quantize(c):
            quantize_state(1, c, up_bf[c])

        out_banks = {}
        out_rows = {}
        out_words = {}
        plane_banks = {}
        out_bf = {}

        def row_tile(q, g, i):
            c, part = place(q)
            if (c, g) not in out_rows:
                out_rows[c, g] = work.tile([P, CHUNKS[c][1] // P, GROUP], F32, name="out_rows", bufs=2)
            return out_rows[c, g][:, 2 * part + i, :]

        def features_in_order(bank):
            return bank[:].rearrange("p (t m) -> p m t", t=PACK)

        def last_update(c, g):
            make_y(tanh_z[0, c, g], c, g)

        def last_gain(c, g):
            make_up(tanh_z[0, c, g], c, g)

        def last_carry(c, g):
            nc.vector.scalar_tensor_tensor(
                out=mid[c, g][:], in0=mid[c, g][:], scalar=16.0 / 9.0, in1=tanh_z[0, c, g][:], op0=ALU.mult, op1=ALU.add
            )

        def last_sum(c, g):
            nc.vector.tensor_tensor(out=tanh_z[1, c, g][:], in0=tanh_z[1, c, g][:], in1=mid[c, g][:], op=ALU.add)

        def last_round(c, g, on_vector):
            out_bf[c, g] = staged("out_bf", [P, CHUNKS[c][1], 2], F32)
            dst = interleaved(as_values(out_bf[c, g][:]), 2)
            src = by_slot(tanh_z[1, c, g][:], 2)
            if on_vector:
                nc.vector.tensor_scalar(out=dst, in0=src, scalar1=0.25, scalar2=None, op0=ALU.mult)
            else:
                nc.scalar.activation(out=dst, in_=src, func=ACT.Copy, scale=0.25)

        def last_turn(q, g, i):
            c, part = place(q)
            out_banks[q, g, i] = new_bank()
            rows = slice((2 * part + i) * P, (2 * part + i + 1) * P)
            for t in range(PACK):
                nc.tensor.transpose(out_banks[q, g, i][:, t * P:(t + 1) * P], tanh_z[1, c, g][:, t, rows], ident[:])

        def last_keep(q, g, i):
            nc.scalar.activation(
                out=row_tile(q, g, i).rearrange("p (m t) -> p m t", t=PACK), in_=features_in_order(out_banks[q, g, i]),
                func=ACT.Copy, scale=0.25,
            )

        def last_store(q, g, i):
            first = q * QUARTER + i * P
            nc.sync.dma_start(out=out_0[first:first + P, g * GROUP:(g + 1) * GROUP], in_=row_tile(q, g, i))

        def out_turn(q, g, i):
            c, part = place(q)
            out_banks[q, g, i] = new_bank()
            rows = slice((2 * part + i) * P, (2 * part + i + 1) * P)
            for t in range(PACK):
                summed = out_banks[q, g, i][:, t * P:(t + 1) * P]
                nc.tensor.matmul(
                    out=summed, lhsT=mid[c, g][:, t, rows], rhs=ident[:], is_transpose=True, start=True, stop=False
                )
                nc.tensor.matmul(
                    out=summed, lhsT=tanh_z[1, c, g][:, t, rows], rhs=ident[:], is_transpose=True, start=False, stop=True
                )

        def out_update(q, g, i):
            c, part = place(q)
            nc.vector.scalar_tensor_tensor(
                out=row_tile(q, g, i).rearrange("p (m t) -> p m t", t=PACK),
                in0=features_in_order(out_banks[q, g, i]),
                scalar=0.25,
                in1=h_rows[c][:, 2 * part + i, g * GROUP:(g + 1) * GROUP].rearrange("p (m t) -> p m t", t=PACK),
                op0=ALU.mult, op1=ALU.add,
            )

        def out_store(q, g):
            c, part = place(q)
            nc.sync.dma_start(
                out=out_0[rows_of(q), g * GROUP:(g + 1) * GROUP].rearrange("(i p) d -> p i d", p=P),
                in_=out_rows[c, g][:, 2 * part:2 * part + 2, :],
            )

        def out_round(q, g, quarters):
            c, part = place(q)
            words = work.tile([P, 2, quarters * QUARTER, 2], BF16, name="out_words")
            for k in range(quarters):
                out_words[q + k, g] = words[:].rearrange("p u m e -> p u (m e)").bitcast(F32)[:, :, rows_of(k)]
            src = out_rows[c, g][:, 2 * part:2 * (part + quarters), :].rearrange("p i (m u e) -> p u (i m) e", u=2, e=2)
            nc.scalar.copy(out=words[:], in_=src)

        def plane_turn(q, g):
            plane_banks[q, g] = turn_words(lambda i, u: out_words[q, g][:, u, i * P:(i + 1) * P])

        def plane_keep(q, g):
            c, part = place(q)
            if (c, g) not in out_bf:
                out_bf[c, g] = staged("out_bf", [P, CHUNKS[c][1], 2], F32)
            nc.scalar.copy(
                out=out_bf[c, g][:, rows_of(part), :], in_=plane_banks[q, g][:].rearrange("p (u b) -> p b u", u=2)
            )

        def out_planes(q, g, quarters):
            c, part = place(q)
            cols = slice(q * QUARTER, (q + quarters) * QUARTER)
            codes = work.tile([P, quarters * QUARTER], U32, name="out_codes", align_bytes=64)
            values = out_bf[c, g][:, part * QUARTER:(part + quarters) * QUARTER, :]
            quantize(codes[:], out_plane[:, g, cols], as_values(values))
            nc.sync.dma_start(out=out_1[g].rearrange("p m t -> p (m t)").bitcast(I32)[:, cols], in_=codes[:].bitcast(I32))

        def out_scales(g, engine):
            for quad in range(4):
                engine.dma_start(
                    out=out_2[g, 4 * quad:4 * quad + 4, :].bitcast(I32),
                    in_=out_plane[32 * quad:32 * quad + 4, g, :].bitcast(I32),
                )

        order = [
            (a_turn, 0, 0, 0), (a_direct, 0, 0, 0), (a_finish, 0), (a_turn, 0, 0, 1), (h_turn, 0, 1),
            (a_direct, 0, 0, 1), (a_finish, 1), (h_keep, 0, 1), (a_interleave, 0, 0, ON_SCALAR), (h_turn, 0, 0),
            (h_gain, 0, 0), (a_turn, 1, 0, 0), (h_gain, 0, 1), (a_turn, 1, 0, 1), (x_turn, 0), (h_turn, 1, 0),
            (diff_subtract, 1, 0, 0), (h_keep, 0, 0), (diff_scale, 1, 0, 0), (h_turn, 1, 1),
            (diff_subtract, 1, 0, 1), (diff_scale, 1, 0, 1), (diff_turn, 0), (x_keep, 0), (diff_turn, 2),
            (diff_turned, 0), (x_turn, 1), (win_move_codes,), (x_keep, 1), (a_quantize, 0, 0), (win_move_scales,),
            (h_gain, 1, 1), (h_gain, 1, 0), (diff_turn, 1), (diff_turned, 2), (h_turn, 2, 0), (diff_turn, 3),
            (h_turn, 3, 0), (a_interleave, 1, 0, ON_VECTOR), (a_turn, 1, 1, 0), (h_quantize, 0), (diff_turned, 1),
            (a_quantize, 1, 0), (x_quantize, 0), (diff_turned, 3), (h_gain, 3, 0), (a_interleave, 0, 1, ON_VECTOR),
            (h_turn, 2, 1), (a_direct, 1, 1, 0), (h_gain, 2, 0), (h_gain, 2, 1), (a_turned, 1, 1, 0), (h_turn, 3, 1),
            (a_turn, 1, 1, 1), (h_gain, 3, 1), (a_direct, 1, 1, 1), (a_turned, 1, 1, 1), (h_quantize, 1),
            (h_keep, 1, 0), (z_matmul, 0, 0, 0, 0), (h_quantize, 2), (z_tanh, 0, 0, 0, 0), (z_matmul, 0, 0, 0, 1),
            (z_tanh, 0, 0, 0, 1), (a_subtract, 1, 1), (a_quantize, 0, 1), (a_quantize, 1, 1), (x_turn, 2),
            (x_keep, 2), (z_matmul, 0, 0, 1, 0), (mid_update, 0, 0), (h_keep, 1, 1), (z_matmul, 0, 0, 1, 1),
            (x_quantize, 1), (mid_gain, 0, 0), (z_tanh, 0, 0, 1, 0), (z_tanh, 0, 0, 1, 1), (mid_update, 0, 1),
            (x_turn, 3), (x_keep, 3), (x_quantize, 2), (z_matmul, 0, 1, 1, 0), (mid_gain, 0, 1),
            (z_matmul, 0, 1, 0, 0), (z_tanh, 0, 1, 1, 0), (z_matmul, 0, 1, 1, 1), (h_keep, 2, 0),
            (z_tanh, 0, 1, 1, 1), (z_matmul, 0, 1, 0, 1), (z_tanh, 0, 1, 0, 0), (z_tanh, 0, 1, 0, 1),
            (z_matmul, 0, 2, 1, 0), (z_matmul, 0, 2, 0, 1), (h_halve, 1), (mid_quantize, 0), (mid_update, 1, 0),
            (h_keep, 2, 1), (z_matmul, 0, 2, 0, 0), (z_tanh, 0, 2, 0, 0), (z_tanh, 0, 2, 1, 0), (z_tanh, 0, 2, 0, 1),
            (h_halve, 0), (z_matmul, 0, 2, 1, 1), (z_matmul, 1, 0, 0, 0), (z_tanh, 1, 0, 0, 0), (h_keep, 3, 1),
            (z_matmul, 1, 0, 0, 1), (z_matmul, 1, 0, 1, 0), (last_update, 1, 1), (z_tanh, 1, 0, 0, 1),
            (out_turn, 0, 0, 0), (z_tanh, 1, 0, 1, 0), (mid_gain, 1, 0), (h_keep, 3, 0), (last_gain, 1, 1),
            (out_turn, 1, 0, 0), (last_carry, 1, 1), (z_tanh, 0, 2, 1, 1), (out_turn, 1, 0, 1), (out_turn, 0, 0, 1),
            (mid_quantize, 1), (z_matmul, 1, 1, 1, 0), (z_tanh, 1, 1, 1, 0), (out_update, 0, 0, 0),
            (out_update, 1, 0, 1), (out_update, 1, 0, 0), (out_update, 0, 0, 1), (out_store, 0, 0),
            (z_matmul, 1, 1, 1, 1), (z_tanh, 1, 1, 1, 1), (z_matmul, 1, 0, 1, 1), (last_update, 2, 0),
            (out_round, 0, 0, 2), (z_tanh, 1, 0, 1, 1), (z_matmul, 1, 1, 0, 0), (last_sum, 1, 1),
            (last_turn, 2, 1, 1), (last_turn, 2, 1, 0), (out_store, 1, 0), (last_keep, 2, 1, 0), (last_update, 2, 1),
            (plane_turn, 0, 0), (out_turn, 1, 1, 0), (out_turn, 0, 1, 0), (out_turn, 1, 1, 1), (last_gain, 2, 0),
            (last_keep, 2, 1, 1), (last_gain, 2, 1), (plane_turn, 1, 0), (last_store, 2, 1, 1),
            (out_update, 0, 1, 0), (out_update, 1, 1, 1), (out_update, 1, 1, 0), (plane_keep, 0, 0),
            (last_round, 1, 1, ON_SCALAR), (last_store, 2, 1, 0), (plane_keep, 1, 0), (out_turn, 0, 1, 1),
            (z_matmul, 1, 1, 0, 1), (z_tanh, 1, 1, 0, 0), (z_tanh, 1, 1, 0, 1), (mid_quantize, 2),
            (out_update, 0, 1, 1), (out_store, 0, 1), (out_planes, 2, 1, 1), (out_round, 0, 1, 2),
            (out_turn, 2, 0, 1), (out_turn, 2, 0, 0), (last_carry, 2, 1), (out_store, 1, 1), (out_planes, 0, 0, 2),
            (last_carry, 2, 0), (z_matmul, 1, 2, 1, 0), (z_tanh, 1, 2, 1, 0), (z_matmul, 1, 2, 1, 1),
            (plane_turn, 0, 1), (out_update, 2, 0, 0), (out_update, 2, 0, 1), (out_store, 2, 0),
            (z_tanh, 1, 2, 1, 1), (plane_turn, 1, 1), (z_matmul, 1, 2, 0, 0), (plane_keep, 0, 1), (last_sum, 2, 1),
            (plane_keep, 1, 1), (z_tanh, 1, 2, 0, 0), (out_planes, 0, 1, 2), (z_matmul, 1, 2, 0, 1),
            (last_turn, 3, 1, 0), (z_tanh, 1, 2, 0, 1), (last_turn, 3, 1, 1), (last_keep, 3, 1, 0),
            (last_store, 3, 1, 0), (last_round, 2, 1, ON_VECTOR), (out_round, 2, 0, 1), (last_keep, 3, 1, 1),
            (last_sum, 2, 0), (last_turn, 3, 0, 0), (out_planes, 3, 1, 1), (out_scales, 1, nc.sync),
            (last_store, 3, 1, 1), (plane_turn, 2, 0), (last_turn, 3, 0, 1), (last_keep, 3, 0, 0),
            (last_round, 2, 0, ON_VECTOR), (last_keep, 3, 0, 1), (last_store, 3, 0, 0), (last_store, 3, 0, 1),
            (out_planes, 3, 0, 1), (plane_keep, 2, 0), (out_planes, 2, 0, 1), (out_scales, 0, nc.scalar),
        ]
        ctx.enter_context(tc.manual_schedule())
        for step, *args in order:
            step(*args)
